import numpy as np
import ml_dtypes


def mxq(x, axis, fmt="e4m3"):
    dtype, down = {"e4m3": (ml_dtypes.float8_e4m3fn, 7), "e5m2": (ml_dtypes.float8_e5m2, 14)}[fmt]
    v = np.moveaxis(np.asarray(x, np.float32).astype(ml_dtypes.bfloat16).astype(np.float64), axis, -1)
    blocks = v.reshape(v.shape[:-1] + (-1, 32))
    amax = np.abs(blocks).max(-1, keepdims=True)
    byte = np.maximum(np.where(amax > 0, np.frexp(amax)[1] - 1 + 127, 0) - down, 1)
    scale = np.exp2(byte - 127.0)
    codes = (blocks / scale).astype(np.float32).astype(dtype).astype(np.float64)
    return np.moveaxis((codes * scale).reshape(v.shape), -1, axis)


WIDE = False


def mx_kscale(k):
    if not WIDE:
        return np.ones(k)
    levels = np.array([10, -10, 5, -5, 0])
    if k % 512:
        return np.exp2(np.random.permutation(np.resize(levels, k // 32))).repeat(32)
    a = np.empty((k // 512, 16))
    for p in range(k // 512):
        a[p, :8] = np.random.permutation(np.resize(levels, 8))
        for g in range(8):
            far = levels[np.abs(levels - a[p, g]) >= 10]
            a[p, g + 8] = far[np.random.randint(len(far))]
    return np.exp2(a.ravel()).repeat(32)


def f64(x):
    return np.asarray(x).astype(np.float64)


def striped(idx):
    return np.tile(idx.reshape(-1, 16).T, (8, 1)).astype(np.uint16)


def unstriped(offs):
    return offs[:16].T.reshape(-1).astype(np.int64)


E2M1 = np.array([0.0, 0.5, 1.0, 1.5, 2.0, 3.0, 4.0, 6.0, -0.0, -0.5, -1.0, -1.5, -2.0, -3.0, -4.0, -6.0])


def pack_weight(w, fmt):
    k, n = w.shape
    w = f64(np.asarray(w, np.float32).astype(ml_dtypes.bfloat16)).reshape(k // 32, 32, n)
    amax = np.abs(w).max(1)
    if fmt == "e4m3":
        byte = np.frexp(amax)[1] - 1 + 127 - 7
    else:
        mant, ex = np.frexp(amax / 6.0)
        byte = np.where(mant > 0.5, ex, ex - 1) + 127
    byte = np.clip(np.where(amax > 0, byte, 1), 1, 254)
    scaled = (w * np.exp2(127.0 - byte)[:, None, :]).reshape(k, n).astype(np.float32)
    by_word = np.ascontiguousarray(scaled.reshape(k // 512, 128, 4, n).transpose(0, 1, 3, 2))
    if fmt == "e4m3":
        words = by_word.astype(ml_dtypes.float8_e4m3fn).view(np.uint8)
    else:
        c = by_word.astype(ml_dtypes.float4_e2m1fn).view(np.uint8) & 0xF
        words = (c[..., 0::2] | (c[..., 1::2] << 4)).reshape(k // 512, 128, 2 * n)
    return np.ascontiguousarray(words), np.ascontiguousarray(byte.astype(np.uint8).reshape(k // 512, 16, n))


def unpack_weight(words, scales, fmt):
    g, _, n = scales.shape
    words = np.ascontiguousarray(words).reshape(g, 128, n, -1)
    if fmt == "e4m3":
        vals = words.view(ml_dtypes.float8_e4m3fn).astype(np.float64)
    else:
        nib = np.empty((g, 128, n, 4), np.uint8)
        nib[..., 0::2] = words & 0xF
        nib[..., 1::2] = words >> 4
        vals = E2M1[nib]
    vals = vals * np.repeat(np.exp2(scales.astype(np.float64) - 127.0), 8, axis=1)[..., None]
    return vals.transpose(0, 1, 3, 2).reshape(g * 512, n)


def gelu(v):
    return 0.5 * v * (1.0 + np.tanh(np.sqrt(2.0 / np.pi) * (v + 0.044715 * v**3)))


K, K2, H, N, T, TB, S, T2 = 1024, 512, 1536, 512, 2048, 1024, 512, 1024

def setup_inputs():
    n = np.random.standard_normal
    s = mx_kscale(K)[:, None]
    s2 = mx_kscale(K2)[:, None]
    u = mx_kscale(H)[:, None]
    tab_words, tab_scales = pack_weight(n((K, T)) * s, "e4m3")
    tab2_words, tab2_scales = pack_weight(n((K2, TB)) * s2, "e4m3")
    w3_words, w3_scales = pack_weight(1.5 * n((K2, H)) / np.sqrt(K2) / s2 * u.T, "e2m1")
    w4_words, w4_scales = pack_weight(n((H, N)) / np.sqrt(H) / u, "e4m3")
    return {
        "tab_words": tab_words, "tab_scales": tab_scales,
        "tab2_words": tab2_words, "tab2_scales": tab2_scales,
        "offs": striped(np.random.permutation(T)[:S]),
        "offs2": striped(np.random.permutation(TB)[:S]),
        "offs3": striped(np.random.permutation(T2)[:S]),
        "offs4": striped(np.random.permutation(T2)[:S]),
        "w1": (1.5 * n((K, H)) / np.sqrt(K) / s).astype(np.float32),
        "gain": (np.exp(0.3 * n(H)) * u[:, 0]).astype(np.float32),
        "w2": (0.52 * n((K2, H)) / np.sqrt(K2) / s2).astype(np.float32),
        "w3_words": w3_words, "w3_scales": w3_scales,
        "wg1": np.exp(0.3 * n((128, S))).astype(np.float32),
        "wg2": np.exp(0.3 * n((128, S))).astype(np.float32),
        "tissue": (0.7 * n((H, T2)) * u).astype(np.float32),
        "w4_words": w4_words, "w4_scales": w4_scales,
        "res": n((N, T2)).astype(np.float32)}

def reference(tab_words, tab_scales, tab2_words, tab2_scales, offs, offs2, offs3, offs4, w1, gain, w2,
              w3_words, w3_scales, wg1, wg2, tissue, w4_words, w4_scales, res):
    v = unpack_weight(tab_words, tab_scales, "e4m3")[:, unstriped(offs)]
    v2 = unpack_weight(tab2_words, tab2_scales, "e4m3")[:, unstriped(offs2)]
    d = mxq(f64(w1), 0, "e4m3").T @ v
    h1 = f64(gain)[:, None] * (0.5 * d * (1.0 + np.tanh(0.7978845608028654 * (d + 0.044715 * d ** 3))))
    ph = mxq(f64(w2), 0, "e4m3").T @ v2
    h2 = np.cos(ph) * (unpack_weight(w3_words, w3_scales, "e2m1").T @ v2)
    pa = np.zeros((H, T2))
    pa[:, unstriped(offs3)] = np.tile(f64(wg1), (H // 128, 1)) * h1
    pb = np.zeros((H, T2))
    pb[:, unstriped(offs4)] = np.tile(f64(wg2), (H // 128, 1)) * h2
    z = pa + pb + f64(tissue)
    y = unpack_weight(w4_words, w4_scales, "e4m3").T @ mxq(z, 0, "e4m3")
    return np.maximum(y, f64(res))

@@ -1,0 +1,346 @@
+from contextlib import ExitStack
+
+import concourse.mybir as mybir
+from concourse.masks import make_identity
+
+K, K2, H, N, T, TB, S, T2 = 1024, 512, 1536, 512, 2048, 1024, 512, 1024
+FLOPS = 2 * (K * H * S + 2 * K2 * H * S + H * N * T2)
+
+F32 = mybir.dt.float32
+BF16 = mybir.dt.bfloat16
+I32 = mybir.dt.int32
+U32 = mybir.dt.uint32
+U16 = mybir.dt.uint16
+U8 = mybir.dt.uint8
+FP8X4 = mybir.dt.float8_e4m3fn_x4
+FP4X4 = mybir.dt.float4_e2m1fn_x4
+ACT = mybir.ActivationFunctionType
+ALU = mybir.AluOpType
+
+P = 128
+PASS = 512
+SLICES = H // P
+GROUPS = H // PASS
+HALVES = T2 // PASS
+LEAD = 7
+SIN_RING = 8
+FEAT_RING = 4
+TISSUE_RING = 4
+RAW_RING = 4
+STAGE_RING = 3
+SUM_RING = 4
+
+
+def tile_list_photoacoustic_vessel_scoring_kernel(
+    tc, tab_words, tab_scales, tab2_words, tab2_scales, offs, offs2, offs3, offs4, w1, gain, w2,
+    w3_words, w3_scales, wg1, wg2, tissue, w4_words, w4_scales, res, out,
+):
+    nc = tc.nc
+    with ExitStack() as ctx:
+        sb = ctx.enter_context(tc.tile_pool(name="sb", bufs=1))
+        ps = ctx.enter_context(tc.psum_pool(name="ps", bufs=1))
+
+        def tile(name, cols, dtype):
+            return sb.tile([P, cols], dtype, name=name, align_bytes=64)
+
+        def ring(name, count, cols, dtype):
+            return [tile("%s%d" % (name, i), cols, dtype) for i in range(count)]
+
+        idx1 = tile("idx1", S // 16, U16)
+        idx2 = tile("idx2", S // 16, U16)
+        idx3 = tile("idx3", S // 16, U16)
+        idx4 = tile("idx4", S // 16, U16)
+        tab_w = ring("tab_w", K // PASS, T, U32)
+        tab_s = tile("tab_s", T, U8)
+        tab2_w = tile("tab2_w", TB, U32)
+        tab2_s = tile("tab2_s", TB, U8)
+        v_w = ring("v_w", K // PASS, S, U32)
+        v_s = tile("v_s", S, U8)
+        v2_w = tile("v2_w", S, U32)
+        v2_s = tile("v2_s", S, U8)
+        w3_w = tile("w3_w", 2 * H, U8)
+        w3_s = tile("w3_s", H, U8)
+        w4_w = ring("w4_w", GROUPS, N, U32)
+        w4_s = tile("w4_s", N, U8)
+        wg1_t = tile("wg1_t", S, F32)
+        wg2_t = tile("wg2_t", S, F32)
+        gain_rows = tile("gain_rows", P, F32)
+        gain_t = tile("gain_t", SLICES, F32)
+        ident = tile("ident", P, F32)
+        raw = ring("raw", RAW_RING, 4 * PASS, F32)
+        stage = ring("stage", STAGE_RING, 4 * PASS, BF16)
+        wq_w = ring("wq_w", 3 * GROUPS, PASS, U32)
+        wq_s = ring("wq_s", 3 * GROUPS, PASS, U8)
+        tis = ring("tis", TISSUE_RING, T2, F32)
+        sin2 = ring("sin2", SIN_RING, S, F32)
+        feat = ring("feat", FEAT_RING, S, F32)
+        wave = ring("wave", 2, S, F32)
+        page_a = ring("page_a", 2, T2, F32)
+        page_b = ring("page_b", LEAD, T2, F32)
+        z_t = ring("z_t", HALVES, 4 * PASS, BF16)
+        z_g = ring("z_g", HALVES, 2 * PASS, F32)
+        zq_w = ring("zq_w", GROUPS * HALVES, PASS, U32)
+        zq_s = ring("zq_s", GROUPS * HALVES, PASS, U8)
+        bank = [ps.tile([P, PASS], F32, name="bank%d" % i) for i in range(8)]
+        wave_banks = bank[0:2]
+        phase_banks = bank[2:4]
+        head_banks = bank[0:2] + bank[4:8]
+        sum_banks = bank[2:6]
+        back_banks = bank[6:8]
+
+        def load_scales(dst, src):
+            passes = src.shape[0]
+            nc.vector.memset(dst[:].bitcast(I32), 0)
+            for q in range(4):
+                rows = src[:, 4 * q : 4 * q + 4, :]
+                nc.sync.dma_start(out=dst[32 * q : 32 * q + 4 * passes, :].bitcast(I32), in_=rows.bitcast(I32))
+
+        def load_scales_spread(dst, src):
+            for q in range(4):
+                rows = src[0, 4 * q : 4 * q + 4, :].bitcast(I32)
+                nc.sync.dma_start(out=dst[32 * q : 32 * (q + 1), :].bitcast(I32), in_=rows.partition_broadcast(8))
+
+        def load_words(dst, src):
+            nc.sync.dma_start(out=dst[:].bitcast(I32), in_=src.rearrange("p t i -> p (t i)").bitcast(I32))
+
+        def block_rows(j):
+            if j < GROUPS:
+                return w2[:, j * PASS : (j + 1) * PASS]
+            g, a = divmod(j - GROUPS, 2)
+            return w1[a * PASS : (a + 1) * PASS, g * PASS : (g + 1) * PASS]
+
+        def load_block(j, c0=0, c1=PASS):
+            dst = raw[j % RAW_RING][:, 4 * c0 : 4 * c1].rearrange("p (t c) -> p t c", t=4)
+            nc.sync.dma_start(out=dst, in_=block_rows(j)[:, c0:c1].rearrange("(p t) c -> p t c", t=4))
+
+        def quantise_block(j, c0=0, c1=PASS):
+            src = raw[j % RAW_RING][:, 4 * c0 : 4 * c1].rearrange("p (t c i) -> p c t i", t=4, i=4)
+            grouped = stage[j % STAGE_RING][:, 4 * c0 : 4 * c1]
+            copy = nc.vector.tensor_copy if (j, c0) == (0, 0) else nc.scalar.copy
+            copy(out=grouped.rearrange("p (c i t) -> p c t i", i=4, t=4), in_=src)
+            nc.vector.quantize_mx(out=wq_w[j][:, c0:c1].bitcast(FP8X4), scales=wq_s[j][:, c0:c1], in_=grouped)
+
+        def load_tissue(s):
+            nc.sync.dma_start(out=tis[s % TISSUE_RING][:], in_=tissue[s * P : (s + 1) * P, :])
+
+        def phase(s):
+            g, c = divmod(s, 4)
+            cols = slice(c * P, (c + 1) * P)
+            acc = phase_banks[s % 2]
+            nc.tensor.matmul_mx(out=acc[:], lhsT=wq_w[g][:, cols].bitcast(FP8X4), lhsT_scale=wq_s[g][:, cols],
+                                rhs=v2_w[:].bitcast(FP8X4), rhs_scale=v2_s[:], start=True, stop=True)
+            dst = sin2[s % SIN_RING]
+            sine = stage[0][:].bitcast(F32)[:, S : 2 * S] if s == 0 else dst[:]
+            nc.scalar.activation(out=sine, in_=acc[:], func=ACT.Sin, scale=0.5)
+            nc.scalar.activation(out=dst[:], in_=sine, func=ACT.Square)
+
+        last_head_block = GROUPS + 1
+
+        def wave_tile(s):
+            if LEAD - 2 <= s < LEAD:
+                k = s - (LEAD - 2)
+                return stage[last_head_block % STAGE_RING][:].bitcast(F32)[:, k * S : (k + 1) * S]
+            if s == 1:
+                return stage[0][:].bitcast(F32)[:, S : 2 * S]
+            return wave[s % 2][:]
+
+        def product(s):
+            acc = head_banks[s % len(head_banks)] if s < LEAD else wave_banks[s % 2]
+            nc.tensor.matmul_mx(out=acc[:], lhsT=w3_w[:, 2 * s * P : 2 * (s + 1) * P].bitcast(FP4X4),
+                                lhsT_scale=w3_s[:, s * P : (s + 1) * P],
+                                rhs=v2_w[:].bitcast(FP8X4), rhs_scale=v2_s[:], start=True, stop=True)
+            nc.vector.scalar_tensor_tensor(out=wave_tile(s), in0=sin2[s % SIN_RING][:], scalar=-0.5, in1=acc[:],
+                                           op0=ALU.add, op1=ALU.mult)
+
+        def page_b_of(s):
+            return page_b[s] if s < LEAD else page_b_of(2 * (s - LEAD) + 1)
+
+        def place_b(s):
+            page = page_b_of(s)
+            if s < LEAD:
+                engine = nc.vector if s < 2 else nc.gpsimd
+                engine.memset(page[:].bitcast(I32), 0)
+            nc.vector.tensor_tensor(page[:].indirect(idx4[:]), wave_tile(s), wg2_t[:], ALU.mult)
+
+        def feature(s):
+            g, c = divmod(s, 4)
+            cols = slice(c * P, (c + 1) * P)
+            acc = back_banks[s % 2]
+            for a in range(2):
+                j = GROUPS + 2 * g + a
+                nc.tensor.matmul_mx(out=acc[:], lhsT=wq_w[j][:, cols].bitcast(FP8X4), lhsT_scale=wq_s[j][:, cols],
+                                    rhs=v_w[a][:].bitcast(FP8X4), rhs_scale=v_s[4 * a : P, :],
+                                    start=(a == 0), stop=(a == 1))
+            dst = feat[s % FEAT_RING]
+            nc.scalar.activation(out=dst[:], in_=acc[:], func=ACT.Gelu_apprx_tanh)
+            nc.scalar.activation(out=dst[:], in_=dst[:], func=ACT.Copy, scale=gain_t[:, s : s + 1])
+
+        def place_a(s):
+            page = page_a[s % 2]
+            if s < 2:
+                nc.gpsimd.memset(page[:].bitcast(I32), 0)
+            nc.vector.tensor_tensor(page[:].indirect(idx3[:]), feat[s % FEAT_RING][:], wg1_t[:], ALU.mult)
+
+        def add_transposed(s, h, src, start, stop):
+            acc = sum_banks[(HALVES * s + h) % SUM_RING]
+            for q in range(4):
+                j0 = h * PASS + q * P
+                nc.tensor.matmul(out=acc[:, q * P : (q + 1) * P], lhsT=src[:, j0 : j0 + P], rhs=ident[:],
+                                 start=(start and q == 0), stop=(stop and q == 3), is_transpose=True)
+
+        def sum_pages(s):
+            for h in range(HALVES):
+                add_transposed(s, h, tis[s % TISSUE_RING], True, False)
+                add_transposed(s, h, page_b_of(s), False, False)
+            for h in range(HALVES):
+                add_transposed(s, h, page_a[s % 2], False, True)
+                acc = sum_banks[(HALVES * s + h) % SUM_RING]
+                c = s % 4
+                src = acc[:].rearrange("j (q p u e) -> j q u p e", q=4, u=2, e=2)
+                dst = z_t[h][:].rearrange("j (q u p e) -> j q u p e", q=4, u=2, e=2)[:, :, :, 32 * c : 32 * (c + 1), :]
+                if s == SLICES - 1 and h == 1:
+                    nc.vector.tensor_copy(out=dst, in_=src)
+                else:
+                    nc.scalar.copy(out=dst, in_=src)
+
+        def turn_back(g, h):
+            words = z_t[h][:].bitcast(F32)
+            for pair in range(2):
+                acc = (bank[4:6] if g == GROUPS - 1 else back_banks)[pair]
+                for k in range(4):
+                    w0 = (4 * pair + k) * P
+                    nc.tensor.transpose(out=acc[:, k * P : (k + 1) * P], in_=words[:, w0 : w0 + P], identity=ident[:])
+                src = acc[:].rearrange("p (q u j) -> p q j u", q=2, u=2)
+                dst = z_g[h][:, pair * PASS : (pair + 1) * PASS].rearrange("p (q j u) -> p q j u", q=2, u=2)
+                if g == GROUPS - 1 and pair == 1 and h == 0:
+                    nc.vector.tensor_copy(out=dst, in_=src)
+                else:
+                    nc.scalar.copy(out=dst, in_=src)
+            nc.vector.quantize_mx(out=zq_w[HALVES * g + h][:].bitcast(FP8X4), scales=zq_s[HALVES * g + h][:],
+                                  in_=z_g[h][:].bitcast(BF16))
+
+        score_banks = [[bank[0], bank[1], bank[2], bank[3]], [bank[6], bank[7], bank[4], bank[5]]]
+
+        def score(n, h, passes):
+            cols = slice(n * P, (n + 1) * P)
+            for g in passes:
+                nc.tensor.matmul_mx(out=score_banks[h][n][:], lhsT=w4_w[g][:, cols].bitcast(FP8X4),
+                                    lhsT_scale=w4_s[4 * g : P, cols],
+                                    rhs=zq_w[HALVES * g + h][:].bitcast(FP8X4), rhs_scale=zq_s[HALVES * g + h][:],
+                                    start=(g == 0), stop=(g == GROUPS - 1))
+
+        def res_tile(n):
+            return raw[1 + n // 2][:, (n % 2) * T2 : (n % 2 + 1) * T2]
+
+        def finish(n, h):
+            cols = slice(h * PASS, (h + 1) * PASS)
+            dst = tis[n][:, cols]
+            nc.vector.tensor_tensor(out=dst, in0=score_banks[h][n][:], in1=res_tile(n)[:, cols], op=ALU.max)
+            nc.sync.dma_start(out=out[n * P : (n + 1) * P, cols], in_=dst)
+
+        nc.sync.dma_start(out=idx2[:], in_=offs2)
+        load_words(tab2_w, tab2_words[0])
+        load_scales_spread(tab2_s, tab2_scales)
+        load_block(0, 0, 2 * P)
+        nc.sync.dma_start(out=w3_w[:].bitcast(I32), in_=w3_words[0].bitcast(I32))
+        load_scales_spread(w3_s, w3_scales)
+        nc.sync.dma_start(out=wg2_t[:], in_=wg2)
+        nc.sync.dma_start(out=idx4[:], in_=offs4)
+        load_block(0, 2 * P, PASS)
+        load_block(1)
+        load_block(2)
+        nc.sync.dma_start(out=idx1[:], in_=offs)
+        for a in range(K // PASS):
+            load_words(tab_w[a], tab_words[a])
+        load_scales(tab_s, tab_scales)
+        load_block(3)
+        make_identity(nc, ident[:])
+
+        quantise_block(0, 0, 2 * P)
+        nc.vector.tensor_copy(v2_w[:], tab2_w[:].indirect(idx2[:]))
+        nc.vector.tensor_copy(v2_s[:], tab2_s[:].indirect(idx2[:]))
+        phase(0)
+        nc.vector.tensor_scalar_mul(out=wg2_t[:], in0=wg2_t[:], scalar1=-2.0)
+        product(0)
+        place_b(0)
+        phase(1)
+        quantise_block(0, 2 * P, PASS)
+        load_block(4)
+        nc.sync.dma_start(out=wg1_t[:], in_=wg1)
+        nc.gpsimd.memset(gain_rows[:], 0.0)
+        nc.sync.dma_start(out=gain_rows[0:SLICES, :], in_=gain.rearrange("(s p) -> s p", p=P))
+        nc.sync.dma_start(out=idx3[:], in_=offs3)
+        load_tissue(0)
+        load_tissue(1)
+        product(1)
+        place_b(1)
+        quantise_block(1)
+        load_block(5)
+        quantise_block(2)
+        load_block(6)
+        load_tissue(2)
+        load_tissue(3)
+        for s in range(2, LEAD - 2):
+            phase(s)
+            product(s)
+            place_b(s)
+        for a in range(K // PASS):
+            nc.vector.tensor_copy(v_w[a][:], tab_w[a][:].indirect(idx1[:]))
+        nc.vector.tensor_copy(v_s[:], tab_s[:].indirect(idx1[:]))
+        nc.tensor.transpose(out=back_banks[0][:, 0:P], in_=gain_rows[:], identity=ident[:])
+        nc.scalar.copy(out=gain_t[:], in_=back_banks[0][:, 0:SLICES])
+        quantise_block(3)
+        load_block(7)
+        quantise_block(4)
+        load_block(8)
+        for s in range(LEAD - 2, SLICES):
+            phase(s)
+        for g in range(GROUPS):
+            load_words(w4_w[g], w4_words[g])
+        load_scales(w4_s, w4_scales)
+        quantise_block(5)
+        quantise_block(6)
+        for s in range(LEAD - 2, LEAD):
+            product(s)
+            place_b(s)
+        for s in range(FEAT_RING):
+            feature(s)
+        for i in range(2):
+            nc.sync.dma_start(out=raw[1 + i][:].rearrange("p (a j) -> p a j", a=2),
+                              in_=res[2 * i * P : 2 * (i + 1) * P, :].rearrange("(a p) j -> p a j", p=P))
+
+        for s in range(SLICES):
+            late = LEAD - 1 + s // 2
+            has_late = s % 2 == 0 and s > 0
+            if has_late:
+                product(late)
+            if s == SLICES - 2:
+                for n in range(2):
+                    for h in range(HALVES):
+                        score(n, h, range(GROUPS - 1))
+            place_a(s)
+            if has_late:
+                place_b(late)
+            if s % 4 == 0 and s > 0:
+                for h in range(HALVES):
+                    turn_back(s // 4 - 1, h)
+            sum_pages(s)
+            if s + TISSUE_RING < SLICES:
+                load_tissue(s + TISSUE_RING)
+            if s + FEAT_RING < SLICES:
+                feature(s + FEAT_RING)
+            if s in (1, 2):
+                quantise_block(6 + s)
+            if s == SLICES - 2:
+                for n in range(2, 4):
+                    score(n, 0, range(GROUPS - 1))
+
+        last = GROUPS - 1
+        turn_back(last, 0)
+        turn_back(last, 1)
+        for n in range(4):
+            score(n, 0, [last])
+            finish(n, 0)
+        for n in range(4):
+            score(n, 1, [last] if n < 2 else range(GROUPS))
+            finish(n, 1)

@@ -22,13 +22,15 @@ PASS = 512
 SLICES = H // P
 GROUPS = H // PASS
 HALVES = T2 // PASS
-LEAD = 7
+LEAD = 6
 SIN_RING = 8
-FEAT_RING = 4
+DIRECT = 4
+SOURCE_RING = 6
+AHEAD = 3
 TISSUE_RING = 4
 RAW_RING = 4
 STAGE_RING = 3
-SUM_RING = 4
+SUM_RING = 6
 
 
 def tile_list_photoacoustic_vessel_scoring_kernel(
@@ -73,20 +75,24 @@ def tile_list_photoacoustic_vessel_scoring_kernel(
         wq_s = ring("wq_s", 3 * GROUPS, PASS, U8)
         tis = ring("tis", TISSUE_RING, T2, F32)
         sin2 = ring("sin2", SIN_RING, S, F32)
-        feat = ring("feat", FEAT_RING, S, F32)
-        wave = ring("wave", 2, S, F32)
+        source = ring("source", SOURCE_RING, S, F32)
         page_a = ring("page_a", 2, T2, F32)
         page_b = ring("page_b", LEAD, T2, F32)
-        z_t = ring("z_t", HALVES, 4 * PASS, BF16)
+        z_t = ring("z_t", 2 * HALVES, 4 * PASS, BF16)
         z_g = ring("z_g", HALVES, 2 * PASS, F32)
         zq_w = ring("zq_w", GROUPS * HALVES, PASS, U32)
         zq_s = ring("zq_s", GROUPS * HALVES, PASS, U8)
         bank = [ps.tile([P, PASS], F32, name="bank%d" % i) for i in range(8)]
-        wave_banks = bank[0:2]
-        phase_banks = bank[2:4]
-        head_banks = bank[0:2] + bank[4:8]
-        sum_banks = bank[2:6]
-        back_banks = bank[6:8]
+        scalar_banks = bank[6:8]
+        taken = {}
+        turns = []
+
+        def scalar_bank():
+            turns.append(0)
+            return scalar_banks[len(turns) % 2]
+
+        def ring_bank(user):
+            return taken.setdefault(user, bank[len(taken) % SUM_RING])
 
         def load_scales(dst, src):
             passes = src.shape[0]
@@ -116,7 +122,7 @@ def tile_list_photoacoustic_vessel_scoring_kernel(
         def quantise_block(j, c0=0, c1=PASS):
             src = raw[j % RAW_RING][:, 4 * c0 : 4 * c1].rearrange("p (t c i) -> p c t i", t=4, i=4)
             grouped = stage[j % STAGE_RING][:, 4 * c0 : 4 * c1]
-            copy = nc.vector.tensor_copy if (j, c0) == (0, 0) else nc.scalar.copy
+            copy = nc.vector.tensor_copy if j == 0 and c1 < PASS else nc.scalar.copy
             copy(out=grouped.rearrange("p (c i t) -> p c t i", i=4, t=4), in_=src)
             nc.vector.quantize_mx(out=wq_w[j][:, c0:c1].bitcast(FP8X4), scales=wq_s[j][:, c0:c1], in_=grouped)
 
@@ -126,7 +132,7 @@ def tile_list_photoacoustic_vessel_scoring_kernel(
         def phase(s):
             g, c = divmod(s, 4)
             cols = slice(c * P, (c + 1) * P)
-            acc = phase_banks[s % 2]
+            acc = scalar_bank()
             nc.tensor.matmul_mx(out=acc[:], lhsT=wq_w[g][:, cols].bitcast(FP8X4), lhsT_scale=wq_s[g][:, cols],
                                 rhs=v2_w[:].bitcast(FP8X4), rhs_scale=v2_s[:], start=True, stop=True)
             dst = sin2[s % SIN_RING]
@@ -134,26 +140,38 @@ def tile_list_photoacoustic_vessel_scoring_kernel(
             nc.scalar.activation(out=sine, in_=acc[:], func=ACT.Sin, scale=0.5)
             nc.scalar.activation(out=dst[:], in_=sine, func=ACT.Square)
 
-        last_head_block = GROUPS + 1
+        order = [("b", s) for s in range(LEAD)]
+        for s in range(SLICES):
+            order.append(("a", s))
+            if s % 2 == 1:
+                order.append(("b", LEAD + s // 2))
+
+        def source_tile(item):
+            return source[order.index(item) % SOURCE_RING][:]
+
+        def stage_half(j, half):
+            return stage[j % STAGE_RING][:].bitcast(F32)[:, half * S : (half + 1) * S]
+
+        wave_places = {1: stage_half(0, 1), 3: stage_half(4, 0), 4: stage_half(4, 1), 5: stage_half(3, 0),
+                       6: stage_half(6, 0), SLICES - 1: source_tile(("a", SLICES - 1))}
 
         def wave_tile(s):
-            if LEAD - 2 <= s < LEAD:
-                k = s - (LEAD - 2)
-                return stage[last_head_block % STAGE_RING][:].bitcast(F32)[:, k * S : (k + 1) * S]
-            if s == 1:
-                return stage[0][:].bitcast(F32)[:, S : 2 * S]
-            return wave[s % 2][:]
+            return wave_places.get(s, source_tile(("b", s)))
 
-        def product(s):
-            acc = head_banks[s % len(head_banks)] if s < LEAD else wave_banks[s % 2]
+        def amplitude(s):
+            acc = bank[s] if s < DIRECT else scalar_bank()
             nc.tensor.matmul_mx(out=acc[:], lhsT=w3_w[:, 2 * s * P : 2 * (s + 1) * P].bitcast(FP4X4),
                                 lhsT_scale=w3_s[:, s * P : (s + 1) * P],
                                 rhs=v2_w[:].bitcast(FP8X4), rhs_scale=v2_s[:], start=True, stop=True)
-            nc.vector.scalar_tensor_tensor(out=wave_tile(s), in0=sin2[s % SIN_RING][:], scalar=-0.5, in1=acc[:],
-                                           op0=ALU.add, op1=ALU.mult)
+            if s >= DIRECT:
+                nc.scalar.copy(out=source_tile(("b", s)), in_=acc[:])
+
+        def product(s):
+            nc.vector.scalar_tensor_tensor(out=wave_tile(s), in0=sin2[s % SIN_RING][:], scalar=-0.5,
+                                           in1=bank[s][:] if s < DIRECT else source_tile(("b", s)), op0=ALU.add, op1=ALU.mult)
 
         def page_b_of(s):
-            return page_b[s] if s < LEAD else page_b_of(2 * (s - LEAD) + 1)
+            return page_b[s] if s < LEAD else page_b_of(2 * (s - LEAD))
 
         def place_b(s):
             page = page_b_of(s)
@@ -165,48 +183,57 @@ def tile_list_photoacoustic_vessel_scoring_kernel(
         def feature(s):
             g, c = divmod(s, 4)
             cols = slice(c * P, (c + 1) * P)
-            acc = back_banks[s % 2]
+            acc = scalar_bank()
             for a in range(2):
                 j = GROUPS + 2 * g + a
                 nc.tensor.matmul_mx(out=acc[:], lhsT=wq_w[j][:, cols].bitcast(FP8X4), lhsT_scale=wq_s[j][:, cols],
                                     rhs=v_w[a][:].bitcast(FP8X4), rhs_scale=v_s[4 * a : P, :],
                                     start=(a == 0), stop=(a == 1))
-            dst = feat[s % FEAT_RING]
-            nc.scalar.activation(out=dst[:], in_=acc[:], func=ACT.Gelu_apprx_tanh)
-            nc.scalar.activation(out=dst[:], in_=dst[:], func=ACT.Copy, scale=gain_t[:, s : s + 1])
+            dst = source_tile(("a", s))
+            nc.scalar.activation(out=dst, in_=acc[:], func=ACT.Gelu_apprx_tanh)
+            nc.scalar.activation(out=dst, in_=dst, func=ACT.Copy, scale=gain_t[:, s : s + 1])
+
+        def prepare(item):
+            (feature if item[0] == "a" else amplitude)(item[1])
 
         def place_a(s):
             page = page_a[s % 2]
             if s < 2:
                 nc.gpsimd.memset(page[:].bitcast(I32), 0)
-            nc.vector.tensor_tensor(page[:].indirect(idx3[:]), feat[s % FEAT_RING][:], wg1_t[:], ALU.mult)
+            nc.vector.tensor_tensor(page[:].indirect(idx3[:]), source_tile(("a", s)), wg1_t[:], ALU.mult)
 
         def add_transposed(s, h, src, start, stop):
-            acc = sum_banks[(HALVES * s + h) % SUM_RING]
+            acc = ring_bank(("sum", s, h))
             for q in range(4):
                 j0 = h * PASS + q * P
                 nc.tensor.matmul(out=acc[:, q * P : (q + 1) * P], lhsT=src[:, j0 : j0 + P], rhs=ident[:],
                                  start=(start and q == 0), stop=(stop and q == 3), is_transpose=True)
 
-        def sum_pages(s):
+        def pages_in_order(s):
+            pages = [page_b_of(s), page_a[s % 2]]
+            return pages if s < SLICES - 1 else pages[::-1]
+
+        def open_sum(s):
             for h in range(HALVES):
                 add_transposed(s, h, tis[s % TISSUE_RING], True, False)
-                add_transposed(s, h, page_b_of(s), False, False)
+                add_transposed(s, h, pages_in_order(s)[0], False, False)
+            if s + TISSUE_RING < SLICES:
+                load_tissue(s + TISSUE_RING)
+
+        def close_sum(s):
+            late = pages_in_order(s)[1]
             for h in range(HALVES):
-                add_transposed(s, h, page_a[s % 2], False, True)
-                acc = sum_banks[(HALVES * s + h) % SUM_RING]
+                add_transposed(s, h, late, False, True)
+                acc = ring_bank(("sum", s, h))
                 c = s % 4
                 src = acc[:].rearrange("j (q p u e) -> j q u p e", q=4, u=2, e=2)
-                dst = z_t[h][:].rearrange("j (q u p e) -> j q u p e", q=4, u=2, e=2)[:, :, :, 32 * c : 32 * (c + 1), :]
-                if s == SLICES - 1 and h == 1:
-                    nc.vector.tensor_copy(out=dst, in_=src)
-                else:
-                    nc.scalar.copy(out=dst, in_=src)
+                dst = z_t[HALVES * (s // 4 % 2) + h][:].rearrange("j (q u p e) -> j q u p e", q=4, u=2, e=2)[:, :, :, 32 * c : 32 * (c + 1), :]
+                nc.scalar.copy(out=dst, in_=src)
 
         def turn_back(g, h):
-            words = z_t[h][:].bitcast(F32)
+            words = z_t[HALVES * (g % 2) + h][:].bitcast(F32)
             for pair in range(2):
-                acc = (bank[4:6] if g == GROUPS - 1 else back_banks)[pair]
+                acc = ring_bank(("sum", SLICES - 1, pair)) if g == GROUPS - 1 else scalar_bank()
                 for k in range(4):
                     w0 = (4 * pair + k) * P
                     nc.tensor.transpose(out=acc[:, k * P : (k + 1) * P], in_=words[:, w0 : w0 + P], identity=ident[:])
@@ -219,12 +246,15 @@ def tile_list_photoacoustic_vessel_scoring_kernel(
             nc.vector.quantize_mx(out=zq_w[HALVES * g + h][:].bitcast(FP8X4), scales=zq_s[HALVES * g + h][:],
                                   in_=z_g[h][:].bitcast(BF16))
 
-        score_banks = [[bank[0], bank[1], bank[2], bank[3]], [bank[6], bank[7], bank[4], bank[5]]]
+        def score_bank(n, h):
+            if h == 0:
+                return ([ring_bank(("sum", SLICES - 3, pair)) for pair in range(2)] + scalar_banks)[n]
+            return ring_bank(("sum", SLICES - 2 + n // 2, n % 2))
 
         def score(n, h, passes):
             cols = slice(n * P, (n + 1) * P)
             for g in passes:
-                nc.tensor.matmul_mx(out=score_banks[h][n][:], lhsT=w4_w[g][:, cols].bitcast(FP8X4),
+                nc.tensor.matmul_mx(out=score_bank(n, h)[:], lhsT=w4_w[g][:, cols].bitcast(FP8X4),
                                     lhsT_scale=w4_s[4 * g : P, cols],
                                     rhs=zq_w[HALVES * g + h][:].bitcast(FP8X4), rhs_scale=zq_s[HALVES * g + h][:],
                                     start=(g == 0), stop=(g == GROUPS - 1))
@@ -235,17 +265,18 @@ def tile_list_photoacoustic_vessel_scoring_kernel(
         def finish(n, h):
             cols = slice(h * PASS, (h + 1) * PASS)
             dst = tis[n][:, cols]
-            nc.vector.tensor_tensor(out=dst, in0=score_banks[h][n][:], in1=res_tile(n)[:, cols], op=ALU.max)
+            nc.vector.tensor_tensor(out=dst, in0=score_bank(n, h)[:], in1=res_tile(n)[:, cols], op=ALU.max)
             nc.sync.dma_start(out=out[n * P : (n + 1) * P, cols], in_=dst)
 
         nc.sync.dma_start(out=idx2[:], in_=offs2)
+        load_block(0, 0, P)
         load_words(tab2_w, tab2_words[0])
         load_scales_spread(tab2_s, tab2_scales)
-        load_block(0, 0, 2 * P)
-        nc.sync.dma_start(out=w3_w[:].bitcast(I32), in_=w3_words[0].bitcast(I32))
-        load_scales_spread(w3_s, w3_scales)
         nc.sync.dma_start(out=wg2_t[:], in_=wg2)
+        nc.sync.dma_start(out=w3_w[:].bitcast(I32), in_=w3_words[0].bitcast(I32))
         nc.sync.dma_start(out=idx4[:], in_=offs4)
+        load_scales_spread(w3_s, w3_scales)
+        load_block(0, P, 2 * P)
         load_block(0, 2 * P, PASS)
         load_block(1)
         load_block(2)
@@ -256,11 +287,13 @@ def tile_list_photoacoustic_vessel_scoring_kernel(
         load_block(3)
         make_identity(nc, ident[:])
 
-        quantise_block(0, 0, 2 * P)
+        quantise_block(0, 0, P)
         nc.vector.tensor_copy(v2_w[:], tab2_w[:].indirect(idx2[:]))
         nc.vector.tensor_copy(v2_s[:], tab2_s[:].indirect(idx2[:]))
         phase(0)
+        quantise_block(0, P, 2 * P)
         nc.vector.tensor_scalar_mul(out=wg2_t[:], in0=wg2_t[:], scalar1=-2.0)
+        amplitude(0)
         product(0)
         place_b(0)
         phase(1)
@@ -272,6 +305,7 @@ def tile_list_photoacoustic_vessel_scoring_kernel(
         nc.sync.dma_start(out=idx3[:], in_=offs3)
         load_tissue(0)
         load_tissue(1)
+        amplitude(1)
         product(1)
         place_b(1)
         quantise_block(1)
@@ -280,60 +314,70 @@ def tile_list_photoacoustic_vessel_scoring_kernel(
         load_block(6)
         load_tissue(2)
         load_tissue(3)
-        for s in range(2, LEAD - 2):
-            phase(s)
-            product(s)
-            place_b(s)
+        phase(2)
+        amplitude(2)
+        product(2)
+        place_b(2)
         for a in range(K // PASS):
             nc.vector.tensor_copy(v_w[a][:], tab_w[a][:].indirect(idx1[:]))
         nc.vector.tensor_copy(v_s[:], tab_s[:].indirect(idx1[:]))
-        nc.tensor.transpose(out=back_banks[0][:, 0:P], in_=gain_rows[:], identity=ident[:])
-        nc.scalar.copy(out=gain_t[:], in_=back_banks[0][:, 0:SLICES])
         quantise_block(3)
         load_block(7)
         quantise_block(4)
         load_block(8)
-        for s in range(LEAD - 2, SLICES):
+        for s in range(3, LEAD):
             phase(s)
+            amplitude(s)
+            product(s)
+            place_b(s)
+        for s in range(LEAD, SLICES):
+            phase(s)
+        gain_bank = scalar_bank()
+        nc.tensor.transpose(out=gain_bank[:, 0:P], in_=gain_rows[:], identity=ident[:])
+        nc.scalar.copy(out=gain_t[:], in_=gain_bank[:, 0:SLICES])
         for g in range(GROUPS):
             load_words(w4_w[g], w4_words[g])
         load_scales(w4_s, w4_scales)
+        feature(0)
+        feature(1)
         quantise_block(5)
         quantise_block(6)
-        for s in range(LEAD - 2, LEAD):
-            product(s)
-            place_b(s)
-        for s in range(FEAT_RING):
-            feature(s)
+        for item in order[LEAD + 2 : LEAD + AHEAD]:
+            prepare(item)
         for i in range(2):
             nc.sync.dma_start(out=raw[1 + i][:].rearrange("p (a j) -> p a j", a=2),
                               in_=res[2 * i * P : 2 * (i + 1) * P, :].rearrange("(a p) j -> p a j", p=P))
 
-        for s in range(SLICES):
-            late = LEAD - 1 + s // 2
-            has_late = s % 2 == 0 and s > 0
-            if has_late:
-                product(late)
-            if s == SLICES - 2:
-                for n in range(2):
-                    for h in range(HALVES):
-                        score(n, h, range(GROUPS - 1))
-            place_a(s)
-            if has_late:
-                place_b(late)
-            if s % 4 == 0 and s > 0:
-                for h in range(HALVES):
-                    turn_back(s // 4 - 1, h)
-            sum_pages(s)
-            if s + TISSUE_RING < SLICES:
-                load_tissue(s + TISSUE_RING)
-            if s + FEAT_RING < SLICES:
-                feature(s + FEAT_RING)
-            if s in (1, 2):
+        open_sum(0)
+        for i in range(LEAD, len(order)):
+            kind, s = order[i]
+            if kind == "a":
+                if s % 2 == 1 and s < SLICES - 1:
+                    product(LEAD + s // 2)
+                place_a(s)
+                if s + 1 < SLICES - 2:
+                    open_sum(s + 1)
+            else:
+                if s == SLICES - 1:
+                    product(s)
+                place_b(s)
+                if s == SLICES - 2:
+                    open_sum(s)
+            if (kind, s) == ("a", SLICES - 1):
+                open_sum(s)
+            if kind == "a" and s < SLICES - 1 or i == len(order) - 1:
+                close_sum(s)
+            if i + AHEAD < len(order):
+                prepare(order[i + AHEAD])
+            if kind == "a" and s >= 4 and s % 4 in (0, 1):
+                turn_back(s // 4 - 1, s % 4 - 0)
+            if kind == "a" and s in (1, 2):
                 quantise_block(6 + s)
-            if s == SLICES - 2:
-                for n in range(2, 4):
+            if (kind, s) == ("a", SLICES - 2):
+                for n in range(0, 4):
                     score(n, 0, range(GROUPS - 1))
+                for n in range(2):
+                    score(n, 1, range(GROUPS - 1))
 
         last = GROUPS - 1
         turn_back(last, 0)

@@ -1,3 +1,4 @@
+import math
 from contextlib import ExitStack
 
 import concourse.mybir as mybir
@@ -26,11 +27,11 @@ LEAD = 6
 SIN_RING = 8
 DIRECT = 4
 SOURCE_RING = 6
-AHEAD = 3
+AHEAD = 4
 TISSUE_RING = 4
 RAW_RING = 4
 STAGE_RING = 3
-SUM_RING = 6
+SUM_RING = 5
 
 
 def tile_list_photoacoustic_vessel_scoring_kernel(
@@ -68,6 +69,7 @@ def tile_list_photoacoustic_vessel_scoring_kernel(
         wg2_t = tile("wg2_t", S, F32)
         gain_rows = tile("gain_rows", P, F32)
         gain_t = tile("gain_t", SLICES, F32)
+        half_pi = tile("half_pi", 1, F32)
         ident = tile("ident", P, F32)
         raw = ring("raw", RAW_RING, 4 * PASS, F32)
         stage = ring("stage", STAGE_RING, 4 * PASS, BF16)
@@ -84,6 +86,7 @@ def tile_list_photoacoustic_vessel_scoring_kernel(
         zq_s = ring("zq_s", GROUPS * HALVES, PASS, U8)
         bank = [ps.tile([P, PASS], F32, name="bank%d" % i) for i in range(8)]
         scalar_banks = bank[6:8]
+        back_bank = bank[5]
         taken = {}
         turns = []
 
@@ -137,8 +140,8 @@ def tile_list_photoacoustic_vessel_scoring_kernel(
                                 rhs=v2_w[:].bitcast(FP8X4), rhs_scale=v2_s[:], start=True, stop=True)
             dst = sin2[s % SIN_RING]
             sine = stage[0][:].bitcast(F32)[:, S : 2 * S] if s == 0 else dst[:]
-            nc.scalar.activation(out=sine, in_=acc[:], func=ACT.Sin, scale=0.5)
-            nc.scalar.activation(out=dst[:], in_=sine, func=ACT.Square)
+            nc.scalar.activation(out=sine, in_=acc[:], func=ACT.Abs)
+            nc.scalar.activation(out=dst[:], in_=sine, func=ACT.Sin, scale=-1.0, bias=half_pi[:, 0:1])
 
         order = [("b", s) for s in range(LEAD)]
         for s in range(SLICES):
@@ -167,8 +170,8 @@ def tile_list_photoacoustic_vessel_scoring_kernel(
                 nc.scalar.copy(out=source_tile(("b", s)), in_=acc[:])
 
         def product(s):
-            nc.vector.scalar_tensor_tensor(out=wave_tile(s), in0=sin2[s % SIN_RING][:], scalar=-0.5,
-                                           in1=bank[s][:] if s < DIRECT else source_tile(("b", s)), op0=ALU.add, op1=ALU.mult)
+            nc.vector.tensor_tensor(out=wave_tile(s), in0=sin2[s % SIN_RING][:],
+                                    in1=bank[s][:] if s < DIRECT else source_tile(("b", s)), op=ALU.mult)
 
         def page_b_of(s):
             return page_b[s] if s < LEAD else page_b_of(2 * (s - LEAD))
@@ -176,8 +179,7 @@ def tile_list_photoacoustic_vessel_scoring_kernel(
         def place_b(s):
             page = page_b_of(s)
             if s < LEAD:
-                engine = nc.vector if s < 2 else nc.gpsimd
-                engine.memset(page[:].bitcast(I32), 0)
+                nc.vector.memset(page[:].bitcast(I32), 0)
             nc.vector.tensor_tensor(page[:].indirect(idx4[:]), wave_tile(s), wg2_t[:], ALU.mult)
 
         def feature(s):
@@ -233,7 +235,7 @@ def tile_list_photoacoustic_vessel_scoring_kernel(
         def turn_back(g, h):
             words = z_t[HALVES * (g % 2) + h][:].bitcast(F32)
             for pair in range(2):
-                acc = ring_bank(("sum", SLICES - 1, pair)) if g == GROUPS - 1 else scalar_bank()
+                acc = ring_bank(("sum", SLICES - 1, pair)) if g == GROUPS - 1 else back_bank
                 for k in range(4):
                     w0 = (4 * pair + k) * P
                     nc.tensor.transpose(out=acc[:, k * P : (k + 1) * P], in_=words[:, w0 : w0 + P], identity=ident[:])
@@ -248,7 +250,7 @@ def tile_list_photoacoustic_vessel_scoring_kernel(
 
         def score_bank(n, h):
             if h == 0:
-                return ([ring_bank(("sum", SLICES - 3, pair)) for pair in range(2)] + scalar_banks)[n]
+                return ([back_bank, ring_bank(("sum", SLICES - 3, 1))] + scalar_banks)[n]
             return ring_bank(("sum", SLICES - 2 + n // 2, n % 2))
 
         def score(n, h, passes):
@@ -272,11 +274,11 @@ def tile_list_photoacoustic_vessel_scoring_kernel(
         load_block(0, 0, P)
         load_words(tab2_w, tab2_words[0])
         load_scales_spread(tab2_s, tab2_scales)
-        nc.sync.dma_start(out=wg2_t[:], in_=wg2)
+        load_block(0, P, 2 * P)
         nc.sync.dma_start(out=w3_w[:].bitcast(I32), in_=w3_words[0].bitcast(I32))
         nc.sync.dma_start(out=idx4[:], in_=offs4)
+        nc.sync.dma_start(out=wg2_t[:], in_=wg2)
         load_scales_spread(w3_s, w3_scales)
-        load_block(0, P, 2 * P)
         load_block(0, 2 * P, PASS)
         load_block(1)
         load_block(2)
@@ -286,13 +288,14 @@ def tile_list_photoacoustic_vessel_scoring_kernel(
         load_scales(tab_s, tab_scales)
         load_block(3)
         make_identity(nc, ident[:])
+        nc.vector.memset(half_pi[:], 1.0)
+        nc.vector.tensor_scalar_mul(out=half_pi[:], in0=half_pi[:], scalar1=math.pi / 2)
 
         quantise_block(0, 0, P)
         nc.vector.tensor_copy(v2_w[:], tab2_w[:].indirect(idx2[:]))
         nc.vector.tensor_copy(v2_s[:], tab2_s[:].indirect(idx2[:]))
         phase(0)
         quantise_block(0, P, 2 * P)
-        nc.vector.tensor_scalar_mul(out=wg2_t[:], in0=wg2_t[:], scalar1=-2.0)
         amplitude(0)
         product(0)
         place_b(0)
@@ -369,8 +372,9 @@ def tile_list_photoacoustic_vessel_scoring_kernel(
                 close_sum(s)
             if i + AHEAD < len(order):
                 prepare(order[i + AHEAD])
-            if kind == "a" and s >= 4 and s % 4 in (0, 1):
-                turn_back(s // 4 - 1, s % 4 - 0)
+            if kind == "b" and s in (7, 9):
+                for h in range(HALVES):
+                    turn_back((s - 7) // 2, h)
             if kind == "a" and s in (1, 2):
                 quantise_block(6 + s)
             if (kind, s) == ("a", SLICES - 2):

@@ -1,4 +1,3 @@
-import math
 from contextlib import ExitStack
 
 import concourse.mybir as mybir
@@ -23,15 +22,12 @@ PASS = 512
 SLICES = H // P
 GROUPS = H // PASS
 HALVES = T2 // PASS
-LEAD = 6
-SIN_RING = 8
-DIRECT = 4
-SOURCE_RING = 6
-AHEAD = 4
+LEAD = 5
+PAGE_RING = 2
+LATE = (9, 10, 11)
+FEAT_RING = 4
 TISSUE_RING = 4
 RAW_RING = 4
-STAGE_RING = 3
-SUM_RING = 5
 
 
 def tile_list_photoacoustic_vessel_scoring_kernel(
@@ -63,43 +59,37 @@ def tile_list_photoacoustic_vessel_scoring_kernel(
         v2_s = tile("v2_s", S, U8)
         w3_w = tile("w3_w", 2 * H, U8)
         w3_s = tile("w3_s", H, U8)
-        w4_w = ring("w4_w", GROUPS, N, U32)
-        w4_s = tile("w4_s", N, U8)
         wg1_t = tile("wg1_t", S, F32)
         wg2_t = tile("wg2_t", S, F32)
         gain_rows = tile("gain_rows", P, F32)
         gain_t = tile("gain_t", SLICES, F32)
-        half_pi = tile("half_pi", 1, F32)
         ident = tile("ident", P, F32)
         raw = ring("raw", RAW_RING, 4 * PASS, F32)
-        stage = ring("stage", STAGE_RING, 4 * PASS, BF16)
+        stage = ring("stage", RAW_RING, 4 * PASS, BF16)
         wq_w = ring("wq_w", 3 * GROUPS, PASS, U32)
         wq_s = ring("wq_s", 3 * GROUPS, PASS, U8)
-        tis = ring("tis", TISSUE_RING, T2, F32)
-        sin2 = ring("sin2", SIN_RING, S, F32)
-        source = ring("source", SOURCE_RING, S, F32)
-        page_a = ring("page_a", 2, T2, F32)
+        w4_w = wq_w[:GROUPS]
+        w4_s = wq_s[GROUPS - 1]
+        tis_pair = ring("tis_pair", TISSUE_RING // 2, 2 * T2, F32)
+        tis = [tis_pair[i // 2][:, i % 2 * T2 : (i % 2 + 1) * T2] for i in range(TISSUE_RING)]
+        landing = raw + [tis_pair[1]] + raw
+        wave = ring("wave", SLICES, S, F32)
+        feat = ring("feat", FEAT_RING, S, F32)
+        page_a = ring("page_a", PAGE_RING, T2, F32)
         page_b = ring("page_b", LEAD, T2, F32)
         z_t = ring("z_t", 2 * HALVES, 4 * PASS, BF16)
         z_g = ring("z_g", HALVES, 2 * PASS, F32)
         zq_w = ring("zq_w", GROUPS * HALVES, PASS, U32)
         zq_s = ring("zq_s", GROUPS * HALVES, PASS, U8)
         bank = [ps.tile([P, PASS], F32, name="bank%d" % i) for i in range(8)]
-        scalar_banks = bank[6:8]
-        back_bank = bank[5]
-        taken = {}
-        turns = []
-
-        def scalar_bank():
-            turns.append(0)
-            return scalar_banks[len(turns) % 2]
-
-        def ring_bank(user):
-            return taken.setdefault(user, bank[len(taken) % SUM_RING])
+        sum_banks = bank[0:4]
+        act_banks = bank[4:6]
+        spare_banks = bank[6:8]
+        phase_banks = act_banks + sum_banks
+        amp_banks = [bank[i] for i in (6, 7, 6, 7, 7, 6, 4, 5, 6, 6, 7, 6)]
 
         def load_scales(dst, src):
             passes = src.shape[0]
-            nc.vector.memset(dst[:].bitcast(I32), 0)
             for q in range(4):
                 rows = src[:, 4 * q : 4 * q + 4, :]
                 nc.sync.dma_start(out=dst[32 * q : 32 * q + 4 * passes, :].bitcast(I32), in_=rows.bitcast(I32))
@@ -112,69 +102,86 @@ def tile_list_photoacoustic_vessel_scoring_kernel(
         def load_words(dst, src):
             nc.sync.dma_start(out=dst[:].bitcast(I32), in_=src.rearrange("p t i -> p (t i)").bitcast(I32))
 
-        def block_rows(j):
-            if j < GROUPS:
-                return w2[:, j * PASS : (j + 1) * PASS]
-            g, a = divmod(j - GROUPS, 2)
-            return w1[a * PASS : (a + 1) * PASS, g * PASS : (g + 1) * PASS]
+        blocks = [[(w2, 0, 0, P), (w2, 0, P, PASS - P)]]
+        blocks.extend([[(w2, 0, g * PASS, PASS)] for g in range(1, GROUPS)])
+        blocks.extend([[(w1, a, g * PASS, PASS)] for g in range(GROUPS) for a in range(2)])
 
-        def load_block(j, c0=0, c1=PASS):
-            dst = raw[j % RAW_RING][:, 4 * c0 : 4 * c1].rearrange("p (t c) -> p t c", t=4)
-            nc.sync.dma_start(out=dst, in_=block_rows(j)[:, c0:c1].rearrange("(p t) c -> p t c", t=4))
+        def piece_columns(j, i):
+            first = sum(piece[3] for piece in blocks[j][:i])
+            return first, first + blocks[j][i][3]
 
-        def quantise_block(j, c0=0, c1=PASS):
-            src = raw[j % RAW_RING][:, 4 * c0 : 4 * c1].rearrange("p (t c i) -> p c t i", t=4, i=4)
-            grouped = stage[j % STAGE_RING][:, 4 * c0 : 4 * c1]
-            copy = nc.vector.tensor_copy if j == 0 and c1 < PASS else nc.scalar.copy
-            copy(out=grouped.rearrange("p (c i t) -> p c t i", i=4, t=4), in_=src)
-            nc.vector.quantize_mx(out=wq_w[j][:, c0:c1].bitcast(FP8X4), scales=wq_s[j][:, c0:c1], in_=grouped)
+        def load_piece(j, i):
+            weight, a, c, width = blocks[j][i]
+            c0, c1 = piece_columns(j, i)
+            dst = landing[j][:, 4 * c0 : 4 * c1].rearrange("p (t c) -> p t c", t=4)
+            rows = weight[a * PASS : (a + 1) * PASS, c : c + width]
+            nc.sync.dma_start(out=dst, in_=rows.rearrange("(p t) c -> p t c", t=4))
+
+        def load_block(j):
+            for i in range(len(blocks[j])):
+                load_piece(j, i)
+
+        def interleave(j, i):
+            c0, c1 = piece_columns(j, i)
+            src = landing[j][:, 4 * c0 : 4 * c1].rearrange("p (t c i) -> p c t i", t=4, i=4)
+            dst = stage[j % RAW_RING][:, 4 * c0 : 4 * c1].rearrange("p (c i t) -> p c t i", i=4, t=4)
+            copy = nc.vector.tensor_copy if j == 0 else nc.scalar.copy
+            copy(out=dst, in_=src)
+
+        def quantise(j, c0, c1):
+            nc.vector.quantize_mx(out=wq_w[j][:, c0:c1].bitcast(FP8X4), scales=wq_s[j][:, c0:c1],
+                                  in_=stage[j % RAW_RING][:, 4 * c0 : 4 * c1])
+
+        def quantise_block(j):
+            for i in range(len(blocks[j])):
+                interleave(j, i)
+            quantise(j, 0, PASS)
+
+        def stationary(first_block, a, s):
+            for j in range(first_block, len(blocks)):
+                for i in range(len(blocks[j])):
+                    c, width = blocks[j][i][2:]
+                    if blocks[j][i][1] == a and c <= s * P < c + width:
+                        c0 = piece_columns(j, i)[0] + s * P - c
+                        return wq_w[j][:, c0 : c0 + P].bitcast(FP8X4), wq_s[j][:, c0 : c0 + P]
 
         def load_tissue(s):
-            nc.sync.dma_start(out=tis[s % TISSUE_RING][:], in_=tissue[s * P : (s + 1) * P, :])
+            nc.sync.dma_start(out=tis[s % TISSUE_RING], in_=tissue[s * P : (s + 1) * P, :])
+
+        def square(s):
+            nc.scalar.activation(out=wave[s][:], in_=wave[s][:], func=ACT.Square)
 
         def phase(s):
-            g, c = divmod(s, 4)
-            cols = slice(c * P, (c + 1) * P)
-            acc = scalar_bank()
-            nc.tensor.matmul_mx(out=acc[:], lhsT=wq_w[g][:, cols].bitcast(FP8X4), lhsT_scale=wq_s[g][:, cols],
+            codes, scales = stationary(0, 0, s)
+            acc = phase_banks[s % len(phase_banks)]
+            nc.tensor.matmul_mx(out=acc[:], lhsT=codes, lhsT_scale=scales,
                                 rhs=v2_w[:].bitcast(FP8X4), rhs_scale=v2_s[:], start=True, stop=True)
-            dst = sin2[s % SIN_RING]
-            sine = stage[0][:].bitcast(F32)[:, S : 2 * S] if s == 0 else dst[:]
-            nc.scalar.activation(out=sine, in_=acc[:], func=ACT.Abs)
-            nc.scalar.activation(out=dst[:], in_=sine, func=ACT.Sin, scale=-1.0, bias=half_pi[:, 0:1])
-
-        order = [("b", s) for s in range(LEAD)]
-        for s in range(SLICES):
-            order.append(("a", s))
-            if s % 2 == 1:
-                order.append(("b", LEAD + s // 2))
-
-        def source_tile(item):
-            return source[order.index(item) % SOURCE_RING][:]
+            nc.scalar.activation(out=wave[s][:], in_=acc[:], func=ACT.Sin, scale=0.5)
+            if s not in LATE:
+                square(s)
 
         def stage_half(j, half):
-            return stage[j % STAGE_RING][:].bitcast(F32)[:, half * S : (half + 1) * S]
+            return stage[j % RAW_RING][:].bitcast(F32)[:, half * S : (half + 1) * S]
 
-        wave_places = {1: stage_half(0, 1), 3: stage_half(4, 0), 4: stage_half(4, 1), 5: stage_half(3, 0),
-                       6: stage_half(6, 0), SLICES - 1: source_tile(("a", SLICES - 1))}
+        wave_places = {2: stage_half(2, 1), 3: stage_half(3, 1), 4: stage_half(4, 1)}
+        gelu_places = {0: stage_half(5, 0), 1: stage_half(5, 1), 2: stage_half(6, 0), 3: stage_half(7, 0),
+                       4: stage_half(8, 0)}
 
         def wave_tile(s):
-            return wave_places.get(s, source_tile(("b", s)))
+            return wave_places.get(s, wave[s][:])
 
-        def amplitude(s):
-            acc = bank[s] if s < DIRECT else scalar_bank()
+        def product(s):
+            acc = amp_banks[s]
             nc.tensor.matmul_mx(out=acc[:], lhsT=w3_w[:, 2 * s * P : 2 * (s + 1) * P].bitcast(FP4X4),
                                 lhsT_scale=w3_s[:, s * P : (s + 1) * P],
                                 rhs=v2_w[:].bitcast(FP8X4), rhs_scale=v2_s[:], start=True, stop=True)
-            if s >= DIRECT:
-                nc.scalar.copy(out=source_tile(("b", s)), in_=acc[:])
-
-        def product(s):
-            nc.vector.tensor_tensor(out=wave_tile(s), in0=sin2[s % SIN_RING][:],
-                                    in1=bank[s][:] if s < DIRECT else source_tile(("b", s)), op=ALU.mult)
+            nc.vector.scalar_tensor_tensor(out=wave_tile(s), in0=wave[s][:], scalar=-0.5, in1=acc[:],
+                                           op0=ALU.add, op1=ALU.mult)
 
         def page_b_of(s):
-            return page_b[s] if s < LEAD else page_b_of(2 * (s - LEAD))
+            if s in LATE:
+                return page_b[s - LATE[0]]
+            return page_b[s] if s < LEAD else page_b_of(s - 2)
 
         def place_b(s):
             page = page_b_of(s)
@@ -183,124 +190,110 @@ def tile_list_photoacoustic_vessel_scoring_kernel(
             nc.vector.tensor_tensor(page[:].indirect(idx4[:]), wave_tile(s), wg2_t[:], ALU.mult)
 
         def feature(s):
-            g, c = divmod(s, 4)
-            cols = slice(c * P, (c + 1) * P)
-            acc = scalar_bank()
+            acc = act_banks[s % 2]
             for a in range(2):
-                j = GROUPS + 2 * g + a
-                nc.tensor.matmul_mx(out=acc[:], lhsT=wq_w[j][:, cols].bitcast(FP8X4), lhsT_scale=wq_s[j][:, cols],
+                codes, scales = stationary(GROUPS, a, s)
+                nc.tensor.matmul_mx(out=acc[:], lhsT=codes, lhsT_scale=scales,
                                     rhs=v_w[a][:].bitcast(FP8X4), rhs_scale=v_s[4 * a : P, :],
                                     start=(a == 0), stop=(a == 1))
-            dst = source_tile(("a", s))
-            nc.scalar.activation(out=dst, in_=acc[:], func=ACT.Gelu_apprx_tanh)
-            nc.scalar.activation(out=dst, in_=dst, func=ACT.Copy, scale=gain_t[:, s : s + 1])
-
-        def prepare(item):
-            (feature if item[0] == "a" else amplitude)(item[1])
+            dst = feat[s % FEAT_RING][:]
+            gelu = gelu_places.get(s, dst)
+            nc.scalar.activation(out=gelu, in_=acc[:], func=ACT.Gelu_apprx_tanh)
+            nc.scalar.activation(out=dst, in_=gelu, func=ACT.Copy, scale=gain_t[:, s : s + 1])
 
         def place_a(s):
-            page = page_a[s % 2]
-            if s < 2:
-                nc.gpsimd.memset(page[:].bitcast(I32), 0)
-            nc.vector.tensor_tensor(page[:].indirect(idx3[:]), source_tile(("a", s)), wg1_t[:], ALU.mult)
+            page = page_a[s % PAGE_RING]
+            if s < PAGE_RING:
+                nc.vector.memset(page[:].bitcast(I32), 0)
+            nc.vector.tensor_tensor(page[:].indirect(idx3[:]), feat[s % FEAT_RING][:], wg1_t[:], ALU.mult)
+
+        def sum_bank(s, h):
+            return sum_banks[HALVES * (s % 2) + h]
 
         def add_transposed(s, h, src, start, stop):
-            acc = ring_bank(("sum", s, h))
+            acc = sum_bank(s, h)
             for q in range(4):
                 j0 = h * PASS + q * P
                 nc.tensor.matmul(out=acc[:, q * P : (q + 1) * P], lhsT=src[:, j0 : j0 + P], rhs=ident[:],
                                  start=(start and q == 0), stop=(stop and q == 3), is_transpose=True)
 
-        def pages_in_order(s):
-            pages = [page_b_of(s), page_a[s % 2]]
-            return pages if s < SLICES - 1 else pages[::-1]
-
-        def open_sum(s):
+        def add_tissue(s):
             for h in range(HALVES):
-                add_transposed(s, h, tis[s % TISSUE_RING], True, False)
-                add_transposed(s, h, pages_in_order(s)[0], False, False)
+                add_transposed(s, h, tis[s % TISSUE_RING], s in LATE, False)
             if s + TISSUE_RING < SLICES:
                 load_tissue(s + TISSUE_RING)
 
-        def close_sum(s):
-            late = pages_in_order(s)[1]
+        def add_page_b(s):
             for h in range(HALVES):
-                add_transposed(s, h, late, False, True)
-                acc = ring_bank(("sum", s, h))
-                c = s % 4
-                src = acc[:].rearrange("j (q p u e) -> j q u p e", q=4, u=2, e=2)
-                dst = z_t[HALVES * (s // 4 % 2) + h][:].rearrange("j (q u p e) -> j q u p e", q=4, u=2, e=2)[:, :, :, 32 * c : 32 * (c + 1), :]
-                nc.scalar.copy(out=dst, in_=src)
+                add_transposed(s, h, page_b_of(s), s not in LATE, False)
+
+        def open_sum(s):
+            add_page_b(s)
+            add_tissue(s)
+
+        def close_sum(s):
+            g, c = divmod(s, 4)
+            for h in range(HALVES):
+                add_transposed(s, h, page_a[s % PAGE_RING], False, True)
+                src = sum_bank(s, h)[:].rearrange("j (q p u e) -> j q u p e", q=4, u=2, e=2)
+                dst = z_t[HALVES * (g % 2) + h][:].rearrange("j (q u p e) -> j q u p e", q=4, u=2, e=2)
+                copy = nc.vector.tensor_copy if (s, h) == (SLICES - 1, 1) else nc.scalar.copy
+                copy(out=dst[:, :, :, 32 * c : 32 * (c + 1), :], in_=src)
 
         def turn_back(g, h):
             words = z_t[HALVES * (g % 2) + h][:].bitcast(F32)
             for pair in range(2):
-                acc = ring_bank(("sum", SLICES - 1, pair)) if g == GROUPS - 1 else back_bank
+                acc = sum_banks[2 + pair] if g == GROUPS - 1 else spare_banks[pair]
                 for k in range(4):
                     w0 = (4 * pair + k) * P
                     nc.tensor.transpose(out=acc[:, k * P : (k + 1) * P], in_=words[:, w0 : w0 + P], identity=ident[:])
                 src = acc[:].rearrange("p (q u j) -> p q j u", q=2, u=2)
                 dst = z_g[h][:, pair * PASS : (pair + 1) * PASS].rearrange("p (q j u) -> p q j u", q=2, u=2)
-                if g == GROUPS - 1 and pair == 1 and h == 0:
-                    nc.vector.tensor_copy(out=dst, in_=src)
-                else:
-                    nc.scalar.copy(out=dst, in_=src)
+                copy = nc.vector.tensor_copy if (g, h, pair) == (GROUPS - 1, 0, 1) else nc.scalar.copy
+                copy(out=dst, in_=src)
             nc.vector.quantize_mx(out=zq_w[HALVES * g + h][:].bitcast(FP8X4), scales=zq_s[HALVES * g + h][:],
                                   in_=z_g[h][:].bitcast(BF16))
 
-        def score_bank(n, h):
-            if h == 0:
-                return ([back_bank, ring_bank(("sum", SLICES - 3, 1))] + scalar_banks)[n]
-            return ring_bank(("sum", SLICES - 2 + n // 2, n % 2))
+        score_banks = [act_banks + spare_banks, sum_banks]
 
         def score(n, h, passes):
             cols = slice(n * P, (n + 1) * P)
             for g in passes:
-                nc.tensor.matmul_mx(out=score_bank(n, h)[:], lhsT=w4_w[g][:, cols].bitcast(FP8X4),
+                nc.tensor.matmul_mx(out=score_banks[h][n][:], lhsT=w4_w[g][:, cols].bitcast(FP8X4),
                                     lhsT_scale=w4_s[4 * g : P, cols],
                                     rhs=zq_w[HALVES * g + h][:].bitcast(FP8X4), rhs_scale=zq_s[HALVES * g + h][:],
                                     start=(g == 0), stop=(g == GROUPS - 1))
 
         def res_tile(n):
-            return raw[1 + n // 2][:, (n % 2) * T2 : (n % 2 + 1) * T2]
+            return raw[n // 2][:, (n % 2) * T2 : (n % 2 + 1) * T2]
+
+        def load_res(i):
+            nc.sync.dma_start(out=raw[i][:].rearrange("p (a j) -> p a j", a=2),
+                              in_=res[2 * i * P : 2 * (i + 1) * P, :].rearrange("(a p) j -> p a j", p=P))
 
         def finish(n, h):
             cols = slice(h * PASS, (h + 1) * PASS)
             dst = tis[n][:, cols]
-            nc.vector.tensor_tensor(out=dst, in0=score_bank(n, h)[:], in1=res_tile(n)[:, cols], op=ALU.max)
+            nc.vector.tensor_tensor(out=dst, in0=score_banks[h][n][:], in1=res_tile(n)[:, cols], op=ALU.max)
             nc.sync.dma_start(out=out[n * P : (n + 1) * P, cols], in_=dst)
 
         nc.sync.dma_start(out=idx2[:], in_=offs2)
-        load_block(0, 0, P)
+        load_piece(0, 0)
         load_words(tab2_w, tab2_words[0])
         load_scales_spread(tab2_s, tab2_scales)
-        load_block(0, P, 2 * P)
+        load_piece(0, 1)
         nc.sync.dma_start(out=w3_w[:].bitcast(I32), in_=w3_words[0].bitcast(I32))
-        nc.sync.dma_start(out=idx4[:], in_=offs4)
-        nc.sync.dma_start(out=wg2_t[:], in_=wg2)
         load_scales_spread(w3_s, w3_scales)
-        load_block(0, 2 * P, PASS)
+        nc.sync.dma_start(out=wg2_t[:], in_=wg2)
+        nc.sync.dma_start(out=idx4[:], in_=offs4)
         load_block(1)
         load_block(2)
         nc.sync.dma_start(out=idx1[:], in_=offs)
         for a in range(K // PASS):
             load_words(tab_w[a], tab_words[a])
+        nc.vector.memset(tab_s[:].bitcast(I32), 0)
         load_scales(tab_s, tab_scales)
         load_block(3)
-        make_identity(nc, ident[:])
-        nc.vector.memset(half_pi[:], 1.0)
-        nc.vector.tensor_scalar_mul(out=half_pi[:], in0=half_pi[:], scalar1=math.pi / 2)
-
-        quantise_block(0, 0, P)
-        nc.vector.tensor_copy(v2_w[:], tab2_w[:].indirect(idx2[:]))
-        nc.vector.tensor_copy(v2_s[:], tab2_s[:].indirect(idx2[:]))
-        phase(0)
-        quantise_block(0, P, 2 * P)
-        amplitude(0)
-        product(0)
-        place_b(0)
-        phase(1)
-        quantise_block(0, 2 * P, PASS)
         load_block(4)
         nc.sync.dma_start(out=wg1_t[:], in_=wg1)
         nc.gpsimd.memset(gain_rows[:], 0.0)
@@ -308,80 +301,97 @@ def tile_list_photoacoustic_vessel_scoring_kernel(
         nc.sync.dma_start(out=idx3[:], in_=offs3)
         load_tissue(0)
         load_tissue(1)
-        amplitude(1)
+        make_identity(nc, ident[:])
+
+        interleave(0, 0)
+        quantise(0, 0, P)
+        nc.vector.tensor_copy(v2_w[:], tab2_w[:].indirect(idx2[:]))
+        nc.vector.tensor_copy(v2_s[:], tab2_s[:].indirect(idx2[:]))
+        phase(0)
+        interleave(0, 1)
+        quantise(0, P, PASS)
+        load_block(5)
+        nc.vector.tensor_scalar_mul(out=wg2_t[:], in0=wg2_t[:], scalar1=-2.0)
+        product(0)
+        place_b(0)
+        for s in range(1, 4):
+            phase(s)
         product(1)
         place_b(1)
         quantise_block(1)
-        load_block(5)
-        quantise_block(2)
         load_block(6)
-        load_tissue(2)
-        load_tissue(3)
-        phase(2)
-        amplitude(2)
-        product(2)
-        place_b(2)
+        quantise_block(2)
+        load_block(7)
         for a in range(K // PASS):
             nc.vector.tensor_copy(v_w[a][:], tab_w[a][:].indirect(idx1[:]))
         nc.vector.tensor_copy(v_s[:], tab_s[:].indirect(idx1[:]))
-        quantise_block(3)
-        load_block(7)
-        quantise_block(4)
-        load_block(8)
-        for s in range(3, LEAD):
+        product(2)
+        place_b(2)
+        for s in range(4, SLICES):
             phase(s)
-            amplitude(s)
+        for s in range(LEAD, LATE[0]):
             product(s)
-            place_b(s)
-        for s in range(LEAD, SLICES):
-            phase(s)
-        gain_bank = scalar_bank()
-        nc.tensor.transpose(out=gain_bank[:, 0:P], in_=gain_rows[:], identity=ident[:])
-        nc.scalar.copy(out=gain_t[:], in_=gain_bank[:, 0:SLICES])
+        nc.tensor.transpose(out=act_banks[0][:, 0:P], in_=gain_rows[:], identity=ident[:])
+        nc.scalar.copy(out=gain_t[:], in_=act_banks[0][:, 0:SLICES])
+        quantise_block(3)
+        load_block(8)
+        product(3)
+        place_b(3)
+        quantise_block(4)
+        load_tissue(2)
+        load_tissue(3)
+        product(4)
+        place_b(4)
+        for s in range(FEAT_RING - 1):
+            feature(s)
+        for s in LATE:
+            square(s)
+        open_sum(0)
+        open_sum(1)
         for g in range(GROUPS):
             load_words(w4_w[g], w4_words[g])
         load_scales(w4_s, w4_scales)
-        feature(0)
-        feature(1)
         quantise_block(5)
         quantise_block(6)
-        for item in order[LEAD + 2 : LEAD + AHEAD]:
-            prepare(item)
-        for i in range(2):
-            nc.sync.dma_start(out=raw[1 + i][:].rearrange("p (a j) -> p a j", a=2),
-                              in_=res[2 * i * P : 2 * (i + 1) * P, :].rearrange("(a p) j -> p a j", p=P))
+        feature(FEAT_RING - 1)
+        load_res(0)
+        load_res(1)
 
-        open_sum(0)
-        for i in range(LEAD, len(order)):
-            kind, s = order[i]
-            if kind == "a":
-                if s % 2 == 1 and s < SLICES - 1:
-                    product(LEAD + s // 2)
-                place_a(s)
-                if s + 1 < SLICES - 2:
-                    open_sum(s + 1)
+        for s in range(LATE[0]):
+            place_a(s)
+            close_sum(s)
+            if s + 2 < LATE[0]:
+                open_sum(s + 2)
             else:
-                if s == SLICES - 1:
-                    product(s)
-                place_b(s)
-                if s == SLICES - 2:
-                    open_sum(s)
-            if (kind, s) == ("a", SLICES - 1):
-                open_sum(s)
-            if kind == "a" and s < SLICES - 1 or i == len(order) - 1:
-                close_sum(s)
-            if i + AHEAD < len(order):
-                prepare(order[i + AHEAD])
-            if kind == "b" and s in (7, 9):
-                for h in range(HALVES):
-                    turn_back((s - 7) // 2, h)
-            if kind == "a" and s in (1, 2):
+                add_tissue(s + 2)
+            if LEAD <= s + 4 < LATE[0]:
+                place_b(s + 4)
+            if s + FEAT_RING < SLICES:
+                feature(s + FEAT_RING)
+            if s in (1, 2):
                 quantise_block(6 + s)
-            if (kind, s) == ("a", SLICES - 2):
-                for n in range(0, 4):
-                    score(n, 0, range(GROUPS - 1))
-                for n in range(2):
-                    score(n, 1, range(GROUPS - 1))
+            if s % 4 == 3:
+                for h in range(HALVES):
+                    turn_back(s // 4, h)
+
+        place_a(LATE[0])
+        place_a(LATE[1])
+        for s in LATE:
+            product(s)
+        for n in range(4):
+            score(n, 0, range(GROUPS - 1))
+        for s in LATE[:2]:
+            place_b(s)
+            add_page_b(s)
+            close_sum(s)
+            if s == LATE[0]:
+                add_tissue(s + 2)
+        place_b(LATE[2])
+        add_page_b(LATE[2])
+        for n in range(2):
+            score(n, 1, range(GROUPS - 1))
+        place_a(LATE[2])
+        close_sum(LATE[2])
 
         last = GROUPS - 1
         turn_back(last, 0)

@@ -151,12 +151,14 @@ def tile_list_photoacoustic_vessel_scoring_kernel(
         def square(s):
             nc.scalar.activation(out=wave[s][:], in_=wave[s][:], func=ACT.Square)
 
-        def phase(s):
+        def sine(s, acc, cols):
             codes, scales = stationary(0, 0, s)
-            acc = phase_banks[s % len(phase_banks)]
-            nc.tensor.matmul_mx(out=acc[:], lhsT=codes, lhsT_scale=scales,
-                                rhs=v2_w[:].bitcast(FP8X4), rhs_scale=v2_s[:], start=True, stop=True)
-            nc.scalar.activation(out=wave[s][:], in_=acc[:], func=ACT.Sin, scale=0.5)
+            nc.tensor.matmul_mx(out=acc[:, cols], lhsT=codes, lhsT_scale=scales,
+                                rhs=v2_w[:, cols].bitcast(FP8X4), rhs_scale=v2_s[:, cols], start=True, stop=True)
+            nc.scalar.activation(out=wave[s][:, cols], in_=acc[:, cols], func=ACT.Sin, scale=0.5)
+
+        def phase(s):
+            sine(s, phase_banks[s % len(phase_banks)], slice(0, S))
             if s not in LATE:
                 square(s)
 
@@ -243,7 +245,7 @@ def tile_list_photoacoustic_vessel_scoring_kernel(
         def turn_back(g, h):
             words = z_t[HALVES * (g % 2) + h][:].bitcast(F32)
             for pair in range(2):
-                acc = sum_banks[2 + pair] if g == GROUPS - 1 else spare_banks[pair]
+                acc = sum_banks[2 * h + pair] if g == GROUPS - 1 else spare_banks[pair]
                 for k in range(4):
                     w0 = (4 * pair + k) * P
                     nc.tensor.transpose(out=acc[:, k * P : (k + 1) * P], in_=words[:, w0 : w0 + P], identity=ident[:])
@@ -278,13 +280,13 @@ def tile_list_photoacoustic_vessel_scoring_kernel(
             nc.sync.dma_start(out=out[n * P : (n + 1) * P, cols], in_=dst)
 
         nc.sync.dma_start(out=idx2[:], in_=offs2)
+        load_scales_spread(tab2_s, tab2_scales)
         load_piece(0, 0)
         load_words(tab2_w, tab2_words[0])
-        load_scales_spread(tab2_s, tab2_scales)
         load_piece(0, 1)
+        nc.sync.dma_start(out=wg2_t[:], in_=wg2)
         nc.sync.dma_start(out=w3_w[:].bitcast(I32), in_=w3_words[0].bitcast(I32))
         load_scales_spread(w3_s, w3_scales)
-        nc.sync.dma_start(out=wg2_t[:], in_=wg2)
         nc.sync.dma_start(out=idx4[:], in_=offs4)
         load_block(1)
         load_block(2)
@@ -303,11 +305,15 @@ def tile_list_photoacoustic_vessel_scoring_kernel(
         load_tissue(1)
         make_identity(nc, ident[:])
 
+        nc.vector.tensor_copy(v2_s[:], tab2_s[:].indirect(idx2[:]))
         interleave(0, 0)
         quantise(0, 0, P)
-        nc.vector.tensor_copy(v2_w[:], tab2_w[:].indirect(idx2[:]))
-        nc.vector.tensor_copy(v2_s[:], tab2_s[:].indirect(idx2[:]))
-        phase(0)
+        for half in range(2):
+            cols = slice(half * S // 2, (half + 1) * S // 2)
+            entries = idx2[:, cols.start // 16 : cols.stop // 16]
+            nc.vector.tensor_copy(v2_w[:, cols], tab2_w[:].indirect(entries))
+            sine(0, phase_banks[-half], cols)
+        square(0)
         interleave(0, 1)
         quantise(0, P, PASS)
         load_block(5)
@@ -388,8 +394,6 @@ def tile_list_photoacoustic_vessel_scoring_kernel(
                 add_tissue(s + 2)
         place_b(LATE[2])
         add_page_b(LATE[2])
-        for n in range(2):
-            score(n, 1, range(GROUPS - 1))
         place_a(LATE[2])
         close_sum(LATE[2])
 
@@ -400,5 +404,5 @@ def tile_list_photoacoustic_vessel_scoring_kernel(
             score(n, 0, [last])
             finish(n, 0)
         for n in range(4):
-            score(n, 1, [last] if n < 2 else range(GROUPS))
+            score(n, 1, range(GROUPS))
             finish(n, 1)

from contextlib import ExitStack

import concourse.mybir as mybir
from concourse.masks import make_identity

K, K2, H, N, T, TB, S, T2 = 1024, 512, 1536, 512, 2048, 1024, 512, 1024
FLOPS = 2 * (K * H * S + 2 * K2 * H * S + H * N * T2)

F32 = mybir.dt.float32
BF16 = mybir.dt.bfloat16
I32 = mybir.dt.int32
U32 = mybir.dt.uint32
U16 = mybir.dt.uint16
U8 = mybir.dt.uint8
FP8X4 = mybir.dt.float8_e4m3fn_x4
FP4X4 = mybir.dt.float4_e2m1fn_x4
ACT = mybir.ActivationFunctionType
ALU = mybir.AluOpType

P = 128
PASS = 512
SLICES = H // P
GROUPS = H // PASS
HALVES = T2 // PASS
LEAD = 5
PAGE_RING = 2
LATE = (9, 10, 11)
FEAT_RING = 4
TISSUE_RING = 4
RAW_RING = 4


def tile_list_photoacoustic_vessel_scoring_kernel(
    tc, tab_words, tab_scales, tab2_words, tab2_scales, offs, offs2, offs3, offs4, w1, gain, w2,
    w3_words, w3_scales, wg1, wg2, tissue, w4_words, w4_scales, res, out,
):
    nc = tc.nc
    with ExitStack() as ctx:
        sb = ctx.enter_context(tc.tile_pool(name="sb", bufs=1))
        ps = ctx.enter_context(tc.psum_pool(name="ps", bufs=1))

        def tile(name, cols, dtype):
            return sb.tile([P, cols], dtype, name=name, align_bytes=64)

        def ring(name, count, cols, dtype):
            return [tile("%s%d" % (name, i), cols, dtype) for i in range(count)]

        idx1 = tile("idx1", S // 16, U16)
        idx2 = tile("idx2", S // 16, U16)
        idx3 = tile("idx3", S // 16, U16)
        idx4 = tile("idx4", S // 16, U16)
        tab_w = ring("tab_w", K // PASS, T, U32)
        tab_s = tile("tab_s", T, U8)
        tab2_w = tile("tab2_w", TB, U32)
        tab2_s = tile("tab2_s", TB, U8)
        v_w = ring("v_w", K // PASS, S, U32)
        v_s = tile("v_s", S, U8)
        v2_w = tile("v2_w", S, U32)
        v2_s = tile("v2_s", S, U8)
        w3_w = tile("w3_w", 2 * H, U8)
        w3_s = tile("w3_s", H, U8)
        wg1_t = tile("wg1_t", S, F32)
        wg2_t = tile("wg2_t", S, F32)
        gain_rows = tile("gain_rows", P, F32)
        gain_t = tile("gain_t", SLICES, F32)
        ident = tile("ident", P, F32)
        raw = ring("raw", RAW_RING, 4 * PASS, F32)
        stage = ring("stage", RAW_RING, 4 * PASS, BF16)
        wq_w = ring("wq_w", 3 * GROUPS, PASS, U32)
        wq_s = ring("wq_s", 3 * GROUPS, PASS, U8)
        w4_w = wq_w[:GROUPS]
        w4_s = wq_s[GROUPS - 1]
        tis_pair = ring("tis_pair", TISSUE_RING // 2, 2 * T2, F32)
        tis = [tis_pair[i // 2][:, i % 2 * T2 : (i % 2 + 1) * T2] for i in range(TISSUE_RING)]
        landing = raw + [tis_pair[1]] + raw
        wave = ring("wave", SLICES, S, F32)
        feat = ring("feat", FEAT_RING, S, F32)
        page_a = ring("page_a", PAGE_RING, T2, F32)
        page_b = ring("page_b", LEAD, T2, F32)
        z_t = ring("z_t", 2 * HALVES, 4 * PASS, BF16)
        z_g = ring("z_g", HALVES, 2 * PASS, F32)
        zq_w = ring("zq_w", GROUPS * HALVES, PASS, U32)
        zq_s = ring("zq_s", GROUPS * HALVES, PASS, U8)
        bank = [ps.tile([P, PASS], F32, name="bank%d" % i) for i in range(8)]
        sum_banks = bank[0:4]
        act_banks = bank[4:6]
        spare_banks = bank[6:8]
        phase_banks = act_banks + sum_banks
        amp_banks = [bank[i] for i in (6, 7, 6, 7, 7, 6, 4, 5, 6, 6, 7, 6)]

        def load_scales(dst, src):
            passes = src.shape[0]
            for q in range(4):
                rows = src[:, 4 * q : 4 * q + 4, :]
                nc.sync.dma_start(out=dst[32 * q : 32 * q + 4 * passes, :].bitcast(I32), in_=rows.bitcast(I32))

        def load_scales_spread(dst, src):
            for q in range(4):
                rows = src[0, 4 * q : 4 * q + 4, :].bitcast(I32)
                nc.sync.dma_start(out=dst[32 * q : 32 * (q + 1), :].bitcast(I32), in_=rows.partition_broadcast(8))

        def load_words(dst, src):
            nc.sync.dma_start(out=dst[:].bitcast(I32), in_=src.rearrange("p t i -> p (t i)").bitcast(I32))

        blocks = [[(w2, 0, 0, P), (w2, 0, P, PASS - P)]]
        blocks.extend([[(w2, 0, g * PASS, PASS)] for g in range(1, GROUPS)])
        blocks.extend([[(w1, a, g * PASS, PASS)] for g in range(GROUPS) for a in range(2)])

        def piece_columns(j, i):
            first = sum(piece[3] for piece in blocks[j][:i])
            return first, first + blocks[j][i][3]

        def load_piece(j, i):
            weight, a, c, width = blocks[j][i]
            c0, c1 = piece_columns(j, i)
            dst = landing[j][:, 4 * c0 : 4 * c1].rearrange("p (t c) -> p t c", t=4)
            rows = weight[a * PASS : (a + 1) * PASS, c : c + width]
            nc.sync.dma_start(out=dst, in_=rows.rearrange("(p t) c -> p t c", t=4))

        def load_block(j):
            for i in range(len(blocks[j])):
                load_piece(j, i)

        def interleave(j, i):
            c0, c1 = piece_columns(j, i)
            src = landing[j][:, 4 * c0 : 4 * c1].rearrange("p (t c i) -> p c t i", t=4, i=4)
            dst = stage[j % RAW_RING][:, 4 * c0 : 4 * c1].rearrange("p (c i t) -> p c t i", i=4, t=4)
            copy = nc.vector.tensor_copy if j == 0 else nc.scalar.copy
            copy(out=dst, in_=src)

        def quantise(j, c0, c1):
            nc.vector.quantize_mx(out=wq_w[j][:, c0:c1].bitcast(FP8X4), scales=wq_s[j][:, c0:c1],
                                  in_=stage[j % RAW_RING][:, 4 * c0 : 4 * c1])

        def quantise_block(j):
            for i in range(len(blocks[j])):
                interleave(j, i)
            quantise(j, 0, PASS)

        def stationary(first_block, a, s):
            for j in range(first_block, len(blocks)):
                for i in range(len(blocks[j])):
                    c, width = blocks[j][i][2:]
                    if blocks[j][i][1] == a and c <= s * P < c + width:
                        c0 = piece_columns(j, i)[0] + s * P - c
                        return wq_w[j][:, c0 : c0 + P].bitcast(FP8X4), wq_s[j][:, c0 : c0 + P]

        def load_tissue(s):
            nc.sync.dma_start(out=tis[s % TISSUE_RING], in_=tissue[s * P : (s + 1) * P, :])

        def square(s):
            nc.scalar.activation(out=wave[s][:], in_=wave[s][:], func=ACT.Square)

        def sine(s, acc, cols):
            codes, scales = stationary(0, 0, s)
            nc.tensor.matmul_mx(out=acc[:, cols], lhsT=codes, lhsT_scale=scales,
                                rhs=v2_w[:, cols].bitcast(FP8X4), rhs_scale=v2_s[:, cols], start=True, stop=True)
            nc.scalar.activation(out=wave[s][:, cols], in_=acc[:, cols], func=ACT.Sin, scale=0.5)

        def phase(s):
            sine(s, phase_banks[s % len(phase_banks)], slice(0, S))
            if s not in LATE:
                square(s)

        def stage_half(j, half):
            return stage[j % RAW_RING][:].bitcast(F32)[:, half * S : (half + 1) * S]

        wave_places = {2: stage_half(2, 1), 3: stage_half(3, 1), 4: stage_half(4, 1)}
        gelu_places = {0: stage_half(5, 0), 1: stage_half(5, 1), 2: stage_half(6, 0), 3: stage_half(7, 0),
                       4: stage_half(8, 0)}

        def wave_tile(s):
            return wave_places.get(s, wave[s][:])

        def product(s):
            acc = amp_banks[s]
            nc.tensor.matmul_mx(out=acc[:], lhsT=w3_w[:, 2 * s * P : 2 * (s + 1) * P].bitcast(FP4X4),
                                lhsT_scale=w3_s[:, s * P : (s + 1) * P],
                                rhs=v2_w[:].bitcast(FP8X4), rhs_scale=v2_s[:], start=True, stop=True)
            nc.vector.scalar_tensor_tensor(out=wave_tile(s), in0=wave[s][:], scalar=-0.5, in1=acc[:],
                                           op0=ALU.add, op1=ALU.mult)

        def page_b_of(s):
            if s in LATE:
                return page_b[s - LATE[0]]
            return page_b[s] if s < LEAD else page_b_of(s - 2)

        def place_b(s):
            page = page_b_of(s)
            if s < LEAD:
                nc.vector.memset(page[:].bitcast(I32), 0)
            nc.vector.tensor_tensor(page[:].indirect(idx4[:]), wave_tile(s), wg2_t[:], ALU.mult)

        def feature(s):
            acc = act_banks[s % 2]
            for a in range(2):
                codes, scales = stationary(GROUPS, a, s)
                nc.tensor.matmul_mx(out=acc[:], lhsT=codes, lhsT_scale=scales,
                                    rhs=v_w[a][:].bitcast(FP8X4), rhs_scale=v_s[4 * a : P, :],
                                    start=(a == 0), stop=(a == 1))
            dst = feat[s % FEAT_RING][:]
            gelu = gelu_places.get(s, dst)
            nc.scalar.activation(out=gelu, in_=acc[:], func=ACT.Gelu_apprx_tanh)
            nc.scalar.activation(out=dst, in_=gelu, func=ACT.Copy, scale=gain_t[:, s : s + 1])

        def place_a(s):
            page = page_a[s % PAGE_RING]
            if s < PAGE_RING:
                nc.vector.memset(page[:].bitcast(I32), 0)
            nc.vector.tensor_tensor(page[:].indirect(idx3[:]), feat[s % FEAT_RING][:], wg1_t[:], ALU.mult)

        def sum_bank(s, h):
            return sum_banks[HALVES * (s % 2) + h]

        def add_transposed(s, h, src, start, stop):
            acc = sum_bank(s, h)
            for q in range(4):
                j0 = h * PASS + q * P
                nc.tensor.matmul(out=acc[:, q * P : (q + 1) * P], lhsT=src[:, j0 : j0 + P], rhs=ident[:],
                                 start=(start and q == 0), stop=(stop and q == 3), is_transpose=True)

        def add_tissue(s):
            for h in range(HALVES):
                add_transposed(s, h, tis[s % TISSUE_RING], s in LATE, False)
            if s + TISSUE_RING < SLICES:
                load_tissue(s + TISSUE_RING)

        def add_page_b(s):
            for h in range(HALVES):
                add_transposed(s, h, page_b_of(s), s not in LATE, False)

        def open_sum(s):
            add_page_b(s)
            add_tissue(s)

        def close_sum(s):
            g, c = divmod(s, 4)
            for h in range(HALVES):
                add_transposed(s, h, page_a[s % PAGE_RING], False, True)
                src = sum_bank(s, h)[:].rearrange("j (q p u e) -> j q u p e", q=4, u=2, e=2)
                dst = z_t[HALVES * (g % 2) + h][:].rearrange("j (q u p e) -> j q u p e", q=4, u=2, e=2)
                copy = nc.vector.tensor_copy if (s, h) == (SLICES - 1, 1) else nc.scalar.copy
                copy(out=dst[:, :, :, 32 * c : 32 * (c + 1), :], in_=src)

        def turn_back(g, h):
            words = z_t[HALVES * (g % 2) + h][:].bitcast(F32)
            for pair in range(2):
                acc = sum_banks[2 * h + pair] if g == GROUPS - 1 else spare_banks[pair]
                for k in range(4):
                    w0 = (4 * pair + k) * P
                    nc.tensor.transpose(out=acc[:, k * P : (k + 1) * P], in_=words[:, w0 : w0 + P], identity=ident[:])
                src = acc[:].rearrange("p (q u j) -> p q j u", q=2, u=2)
                dst = z_g[h][:, pair * PASS : (pair + 1) * PASS].rearrange("p (q j u) -> p q j u", q=2, u=2)
                copy = nc.vector.tensor_copy if (g, h, pair) == (GROUPS - 1, 0, 1) else nc.scalar.copy
                copy(out=dst, in_=src)
            nc.vector.quantize_mx(out=zq_w[HALVES * g + h][:].bitcast(FP8X4), scales=zq_s[HALVES * g + h][:],
                                  in_=z_g[h][:].bitcast(BF16))

        score_banks = [act_banks + spare_banks, sum_banks]

        def score(n, h, passes):
            cols = slice(n * P, (n + 1) * P)
            for g in passes:
                nc.tensor.matmul_mx(out=score_banks[h][n][:], lhsT=w4_w[g][:, cols].bitcast(FP8X4),
                                    lhsT_scale=w4_s[4 * g : P, cols],
                                    rhs=zq_w[HALVES * g + h][:].bitcast(FP8X4), rhs_scale=zq_s[HALVES * g + h][:],
                                    start=(g == 0), stop=(g == GROUPS - 1))

        def res_tile(n):
            return raw[n // 2][:, (n % 2) * T2 : (n % 2 + 1) * T2]

        def load_res(i):
            nc.sync.dma_start(out=raw[i][:].rearrange("p (a j) -> p a j", a=2),
                              in_=res[2 * i * P : 2 * (i + 1) * P, :].rearrange("(a p) j -> p a j", p=P))

        def finish(n, h):
            cols = slice(h * PASS, (h + 1) * PASS)
            dst = tis[n][:, cols]
            nc.vector.tensor_tensor(out=dst, in0=score_banks[h][n][:], in1=res_tile(n)[:, cols], op=ALU.max)
            nc.sync.dma_start(out=out[n * P : (n + 1) * P, cols], in_=dst)

        nc.sync.dma_start(out=idx2[:], in_=offs2)
        load_scales_spread(tab2_s, tab2_scales)
        load_piece(0, 0)
        load_words(tab2_w, tab2_words[0])
        load_piece(0, 1)
        nc.sync.dma_start(out=wg2_t[:], in_=wg2)
        nc.sync.dma_start(out=w3_w[:].bitcast(I32), in_=w3_words[0].bitcast(I32))
        load_scales_spread(w3_s, w3_scales)
        nc.sync.dma_start(out=idx4[:], in_=offs4)
        load_block(1)
        load_block(2)
        nc.sync.dma_start(out=idx1[:], in_=offs)
        for a in range(K // PASS):
            load_words(tab_w[a], tab_words[a])
        nc.vector.memset(tab_s[:].bitcast(I32), 0)
        load_scales(tab_s, tab_scales)
        load_block(3)
        load_block(4)
        nc.sync.dma_start(out=wg1_t[:], in_=wg1)
        nc.gpsimd.memset(gain_rows[:], 0.0)
        nc.sync.dma_start(out=gain_rows[0:SLICES, :], in_=gain.rearrange("(s p) -> s p", p=P))
        nc.sync.dma_start(out=idx3[:], in_=offs3)
        load_tissue(0)
        load_tissue(1)
        make_identity(nc, ident[:])

        nc.vector.tensor_copy(v2_s[:], tab2_s[:].indirect(idx2[:]))
        interleave(0, 0)
        quantise(0, 0, P)
        for half in range(2):
            cols = slice(half * S // 2, (half + 1) * S // 2)
            entries = idx2[:, cols.start // 16 : cols.stop // 16]
            nc.vector.tensor_copy(v2_w[:, cols], tab2_w[:].indirect(entries))
            sine(0, phase_banks[-half], cols)
        square(0)
        interleave(0, 1)
        quantise(0, P, PASS)
        load_block(5)
        nc.vector.tensor_scalar_mul(out=wg2_t[:], in0=wg2_t[:], scalar1=-2.0)
        product(0)
        place_b(0)
        for s in range(1, 4):
            phase(s)
        product(1)
        place_b(1)
        quantise_block(1)
        load_block(6)
        quantise_block(2)
        load_block(7)
        for a in range(K // PASS):
            nc.vector.tensor_copy(v_w[a][:], tab_w[a][:].indirect(idx1[:]))
        nc.vector.tensor_copy(v_s[:], tab_s[:].indirect(idx1[:]))
        product(2)
        place_b(2)
        for s in range(4, SLICES):
            phase(s)
        for s in range(LEAD, LATE[0]):
            product(s)
        nc.tensor.transpose(out=act_banks[0][:, 0:P], in_=gain_rows[:], identity=ident[:])
        nc.scalar.copy(out=gain_t[:], in_=act_banks[0][:, 0:SLICES])
        quantise_block(3)
        load_block(8)
        product(3)
        place_b(3)
        quantise_block(4)
        load_tissue(2)
        load_tissue(3)
        product(4)
        place_b(4)
        for s in range(FEAT_RING - 1):
            feature(s)
        for s in LATE:
            square(s)
        open_sum(0)
        open_sum(1)
        for g in range(GROUPS):
            load_words(w4_w[g], w4_words[g])
        load_scales(w4_s, w4_scales)
        quantise_block(5)
        quantise_block(6)
        feature(FEAT_RING - 1)
        load_res(0)
        load_res(1)

        for s in range(LATE[0]):
            place_a(s)
            close_sum(s)
            if s + 2 < LATE[0]:
                open_sum(s + 2)
            else:
                add_tissue(s + 2)
            if LEAD <= s + 4 < LATE[0]:
                place_b(s + 4)
            if s + FEAT_RING < SLICES:
                feature(s + FEAT_RING)
            if s in (1, 2):
                quantise_block(6 + s)
            if s % 4 == 3:
                for h in range(HALVES):
                    turn_back(s // 4, h)

        place_a(LATE[0])
        place_a(LATE[1])
        for s in LATE:
            product(s)
        for n in range(4):
            score(n, 0, range(GROUPS - 1))
        for s in LATE[:2]:
            place_b(s)
            add_page_b(s)
            close_sum(s)
            if s == LATE[0]:
                add_tissue(s + 2)
        place_b(LATE[2])
        add_page_b(LATE[2])
        place_a(LATE[2])
        close_sum(LATE[2])

        last = GROUPS - 1
        turn_back(last, 0)
        turn_back(last, 1)
        for n in range(4):
            score(n, 0, [last])
            finish(n, 0)
        for n in range(4):
            score(n, 1, range(GROUPS))
            finish(n, 1)
